import numpy as np
import ml_dtypes


def mxq(x, axis, fmt="e4m3"):
    dtype, down = {"e4m3": (ml_dtypes.float8_e4m3fn, 7), "e5m2": (ml_dtypes.float8_e5m2, 14)}[fmt]
    v = np.moveaxis(np.asarray(x, np.float32).astype(ml_dtypes.bfloat16).astype(np.float64), axis, -1)
    blocks = v.reshape(v.shape[:-1] + (-1, 32))
    amax = np.abs(blocks).max(-1, keepdims=True)
    byte = np.maximum(np.where(amax > 0, np.frexp(amax)[1] - 1 + 127, 0) - down, 1)
    scale = np.exp2(byte - 127.0)
    codes = (blocks / scale).astype(np.float32).astype(dtype).astype(np.float64)
    return np.moveaxis((codes * scale).reshape(v.shape), -1, axis)


WIDE = False


def mx_kscale(k):
    if not WIDE:
        return np.ones(k)
    levels = np.array([10, -10, 5, -5, 0])
    if k % 512:
        return np.exp2(np.random.permutation(np.resize(levels, k // 32))).repeat(32)
    a = np.empty((k // 512, 16))
    for p in range(k // 512):
        a[p, :8] = np.random.permutation(np.resize(levels, 8))
        for g in range(8):
            far = levels[np.abs(levels - a[p, g]) >= 10]
            a[p, g + 8] = far[np.random.randint(len(far))]
    return np.exp2(a.ravel()).repeat(32)


def f64(x):
    return np.asarray(x).astype(np.float64)


def striped(idx):
    return np.tile(idx.reshape(-1, 16).T, (8, 1)).astype(np.uint16)


def unstriped(offs):
    return offs[:16].T.reshape(-1).astype(np.int64)


E2M1 = np.array([0.0, 0.5, 1.0, 1.5, 2.0, 3.0, 4.0, 6.0, -0.0, -0.5, -1.0, -1.5, -2.0, -3.0, -4.0, -6.0])


def pack_weight(w, fmt):
    k, n = w.shape
    w = f64(np.asarray(w, np.float32).astype(ml_dtypes.bfloat16)).reshape(k // 32, 32, n)
    amax = np.abs(w).max(1)
    if fmt == "e4m3":
        byte = np.frexp(amax)[1] - 1 + 127 - 7
    else:
        mant, ex = np.frexp(amax / 6.0)
        byte = np.where(mant > 0.5, ex, ex - 1) + 127
    byte = np.clip(np.where(amax > 0, byte, 1), 1, 254)
    scaled = (w * np.exp2(127.0 - byte)[:, None, :]).reshape(k, n).astype(np.float32)
    by_word = np.ascontiguousarray(scaled.reshape(k // 512, 128, 4, n).transpose(0, 1, 3, 2))
    if fmt == "e4m3":
        words = by_word.astype(ml_dtypes.float8_e4m3fn).view(np.uint8)
    else:
        c = by_word.astype(ml_dtypes.float4_e2m1fn).view(np.uint8) & 0xF
        words = (c[..., 0::2] | (c[..., 1::2] << 4)).reshape(k // 512, 128, 2 * n)
    return np.ascontiguousarray(words), np.ascontiguousarray(byte.astype(np.uint8).reshape(k // 512, 16, n))


def unpack_weight(words, scales, fmt):
    g, _, n = scales.shape
    words = np.ascontiguousarray(words).reshape(g, 128, n, -1)
    if fmt == "e4m3":
        vals = words.view(ml_dtypes.float8_e4m3fn).astype(np.float64)
    else:
        nib = np.empty((g, 128, n, 4), np.uint8)
        nib[..., 0::2] = words & 0xF
        nib[..., 1::2] = words >> 4
        vals = E2M1[nib]
    vals = vals * np.repeat(np.exp2(scales.astype(np.float64) - 127.0), 8, axis=1)[..., None]
    return vals.transpose(0, 1, 3, 2).reshape(g * 512, n)


def gelu(v):
    return 0.5 * v * (1.0 + np.tanh(np.sqrt(2.0 / np.pi) * (v + 0.044715 * v**3)))


K, T, E, C, H, N = 2560, 768, 6, 256, 512, 128


def by_expert(wq, xq):
    return np.concatenate([wq[e].T @ xq[:, e * C:(e + 1) * C] for e in range(E)], axis=1)


def setup_inputs():
    n = np.random.standard_normal
    s = mx_kscale(K)[:, None]
    u = mx_kscale(H)
    first = np.random.permutation(np.repeat(np.arange(E), T // E))
    second = (first + 1 + np.random.permutation(np.repeat(np.arange(E - 1), -(-T // (E - 1)))[:T])) % E
    while np.bincount(second, minlength=E).max() != T // E:
        load = np.bincount(second, minlength=E); hi, lo = int(load.argmax()), int(load.argmin())
        t = np.flatnonzero((second == hi) & (first != lo))[0]; second[t] = lo
    slot_token = np.empty(E * C, np.int64); pos = np.empty((2, T), np.int64); fill = np.zeros(E, np.int64)
    place = np.stack([np.random.permutation(C) for _ in range(E)])
    for r, deal in enumerate((first, second)):
        for t in np.random.permutation(T):
            e = deal[t]; j = e * C + place[e, fill[e]]; fill[e] += 1; slot_token[j] = t; pos[r, t] = j
    g = np.random.uniform(0.2, 0.8, T)
    w1 = [pack_weight(m, "e2m1") for m in n((E, K, H)) / np.sqrt(K) / s[None] * u[None, None, :]]
    w2 = [pack_weight(m, "e2m1") for m in n((E, H, N)) / np.sqrt(H) / u[None, :, None]]
    x = pack_weight(n((K, T)) * s, "e4m3")
    return {
        "x_words": x[0],
        "x_scales": x[1],
        "w1_words": np.stack([m[0] for m in w1]),
        "w1_scales": np.stack([m[1] for m in w1]),
        "w2_words": np.stack([m[0] for m in w2]),
        "w2_scales": np.stack([m[1] for m in w2]),
        "gate": np.stack([np.tile(g, (N, 1)), np.tile(1.0 - g, (N, 1))]).astype(np.float32),
        "offs": striped(slot_token),
        "pos1": striped(pos[0]),
        "pos2": striped(pos[1]),
    }


def reference(x_words, x_scales, w1_words, w1_scales, w2_words, w2_scales, gate, offs, pos1, pos2):
    idx = unstriped(offs)
    w1 = np.stack([unpack_weight(w1_words[e], w1_scales[e], "e2m1") for e in range(E)])
    w2 = np.stack([unpack_weight(w2_words[e], w2_scales[e], "e2m1") for e in range(E)])
    xq = unpack_weight(x_words, x_scales, "e4m3")[:, idx]
    h = gelu(by_expert(w1, xq))
    y = by_expert(w2, mxq(h, 0, "e4m3"))
    return f64(gate[0]) * y[:, unstriped(pos1)] + f64(gate[1]) * y[:, unstriped(pos2)]

@@ -1,0 +1,217 @@
+from contextlib import ExitStack
+
+import concourse.mybir as mybir
+from concourse.masks import make_identity
+
+K, T, E, C, H, N = 2560, 768, 6, 256, 512, 128
+S = E * C
+P = 128
+PASSES = K // 512
+FLOPS = 2 * S * (K * H + H * N)
+
+F32 = mybir.dt.float32
+BF16 = mybir.dt.bfloat16
+I32 = mybir.dt.int32
+U32 = mybir.dt.uint32
+U16 = mybir.dt.uint16
+U8 = mybir.dt.uint8
+FP8X4 = mybir.dt.float8_e4m3fn_x4
+FP4X4 = mybir.dt.float4_e2m1fn_x4
+GELU = mybir.ActivationFunctionType.Gelu_apprx_tanh
+MULT = mybir.AluOpType.mult
+ADD = mybir.AluOpType.add
+
+CHUNKS = [(0, 4), (4, 4), (8, 2), (10, 1), (11, 1)]
+HEAD = 512
+QUADS = (0, 2, 1, 3)
+
+
+def tile_moe_pkd_mlp_gelu_kernel(
+    tc, x_words, x_scales, w1_words, w1_scales, w2_words, w2_scales, gate, offs, pos1, pos2, out
+):
+    nc = tc.nc
+    with ExitStack() as ctx:
+        lists = ctx.enter_context(tc.tile_pool(name="lists", bufs=1))
+        keep = ctx.enter_context(tc.tile_pool(name="keep", bufs=1))
+        word_ring = ctx.enter_context(tc.tile_pool(name="word_ring", bufs=4))
+        w1_ring = ctx.enter_context(tc.tile_pool(name="w1_ring", bufs=7))
+        acc_pool = ctx.enter_context(tc.psum_pool(name="acc", bufs=6))
+        turn_pool = ctx.enter_context(tc.psum_pool(name="turn", bufs=2))
+
+        def held(name, shape, dtype):
+            return keep.tile(shape, dtype, name=name, align_bytes=64)
+
+        offs_t = lists.tile([P, S // 16], U16, name="offs_t")
+        pos1_t = lists.tile([P, T // 16], U16, name="pos1_t")
+        pos2_t = lists.tile([P, T // 16], U16, name="pos2_t")
+
+        xs = held("xs", [P, T], U8)
+        xw = [held("xw%d" % a, [P, T], I32) for a in range(PASSES)]
+        plane_head = held("plane_head", [P, 4, HEAD], U8)
+        plane_rest = held("plane_rest", [P, 4, S - HEAD], U8)
+        last_head = held("last_head", [P, HEAD], U8)
+        last_rest = held("last_rest", [P, S - HEAD], U8)
+        w1s_head = held("w1s_head", [P, 2 * PASSES, H], U8)
+        w1s_rest = held("w1s_rest", [P, 4 * PASSES, H], U8)
+        w2s = held("w2s", [P, E, N], U8)
+        w1 = {}
+        w2 = held("w2", [P, E, 2 * N], U8)
+        ident = held("ident", [P, P], F32)
+        y = held("y", [P, S], F32)
+
+        def load_scale_rows(queue, dst, src):
+            rows = src.rearrange("e s (q r) n -> r q (e s) n", r=4)
+            for r in range(4):
+                queue.dma_start(out=dst[r:P:32].bitcast(I32), in_=rows[r].bitcast(I32))
+
+        def load_x(a):
+            nc.sync.dma_start(out=xw[a][:], in_=x_words[a].rearrange("p t r -> p (t r)").bitcast(I32))
+
+        def load_w1(pair, a):
+            w1[pair, a] = w1_ring.tile([P, 2, 2 * H], U8, name="w1", align_bytes=64)
+            nc.sync.dma_start(
+                out=w1[pair, a][:].bitcast(I32),
+                in_=w1_words[2 * pair : 2 * pair + 2, a].rearrange("e p b -> p e b").bitcast(I32),
+            )
+
+        def gather_scales(s0, s1, four, last):
+            gs = keep.tile([P, s1 - s0], U8, name="gs", align_bytes=64)
+            for c in range(s0, s1, HEAD):
+                nc.vector.tensor_copy(
+                    gs[:, c - s0 : c - s0 + HEAD], xs[:].indirect(offs_t[:, c // 16 : (c + HEAD) // 16])
+                )
+            for q in QUADS:
+                nc.scalar.dma_start(
+                    out=four[32 * q : 32 * q + 4].bitcast(I32), in_=gs[16 * q : 16 * q + 16, :].bitcast(I32)
+                )
+            for q in QUADS:
+                nc.scalar.dma_start(
+                    out=last[32 * q : 32 * q + 4, :].bitcast(I32), in_=gs[112 + 4 * q : 116 + 4 * q, :].bitcast(I32)
+                )
+
+        def x_plane(a, j):
+            four, last, s0 = (plane_head, last_head, j * P) if j * P < HEAD else (plane_rest, last_rest, j * P - HEAD)
+            return last[:, s0 : s0 + P] if a == PASSES - 1 else four[:, a, s0 : s0 + P]
+
+        def w1_operand(e, a):
+            words = w1[e // 2, a][:, e % 2, :].bitcast(FP4X4)
+            if e < 2:
+                return words, w1s_head[:, e * PASSES + a, :]
+            return words, w1s_rest[:, (e - 2) * PASSES + a, :]
+
+        nc.vector.memset(xs[64:112, :].bitcast(I32), 0)
+        make_identity(nc, ident[:])
+
+        nc.sync.dma_start(offs_t[:], offs)
+        nc.scalar.dma_start(
+            out=xs[0:64, :].bitcast(I32), in_=x_scales[0:4].rearrange("a f t -> f a t").bitcast(I32)
+        )
+        nc.scalar.dma_start(out=xs[112:P, :].bitcast(I32), in_=x_scales[4].bitcast(I32))
+        load_x(0)
+        load_scale_rows(nc.sync, w1s_head, w1_scales[0:2])
+        load_w1(0, 0)
+        gather_scales(0, HEAD, plane_head, last_head)
+
+        def gather_words(j0, n, a):
+            gw = word_ring.tile([P, n * P], U32, name="gw", align_bytes=64)
+            nc.vector.tensor_copy(gw[:], xw[a][:].bitcast(U32).indirect(offs_t[:, 8 * j0 : 8 * (j0 + n)]))
+            return gw
+
+        def first_layer_pass(accs, j0, n, a, gw):
+            for i in range(n):
+                j = j0 + i
+                w, ws = w1_operand(j // 2, a)
+                nc.tensor.matmul_mx(
+                    out=accs[i][:],
+                    lhsT=gw[:, i * P : (i + 1) * P].bitcast(FP8X4),
+                    lhsT_scale=x_plane(a, j),
+                    rhs=w,
+                    rhs_scale=ws,
+                    start=(a == 0),
+                    stop=(a == PASSES - 1),
+                )
+
+        def activate(j, acc):
+            hb = held("hb%d" % j, [P, H], BF16)
+            nc.scalar.activation(
+                out=hb[:].rearrange("s (u p e) -> s u p e", u=2, e=2),
+                in_=acc[:].rearrange("s (p u e) -> s u p e", u=2, e=2),
+                func=GELU,
+            )
+            return hb
+
+        def turn(hbs, ht):
+            n = len(hbs)
+            turned = turn_pool.tile([P, n, 2, P], F32, name="turned")
+            for i in range(n):
+                words = hbs[i][:].bitcast(F32)
+                for u in range(2):
+                    nc.tensor.transpose(turned[:, i, u, :], words[:, u * P : (u + 1) * P], ident[:])
+            nc.scalar.copy(
+                out=ht.bitcast(F32).rearrange("p (i s u) -> p i s u", i=n, u=2),
+                in_=turned[:].rearrange("p i u s -> p i s u"),
+            )
+
+        hts = []
+        for j0, n in CHUNKS:
+            accs = [acc_pool.tile([P, H], F32, name="acc") for i in range(n)]
+            for a in range(PASSES):
+                if j0 == 0 and a + 1 < PASSES:
+                    load_x(a + 1)
+                    load_w1(0, a + 1)
+                if j0 > 0 and j0 % 4 == 0:
+                    load_w1(j0 // 4, a)
+                gw = gather_words(j0, n, a)
+                if j0 == 0 and a == 1:
+                    gather_scales(HEAD, S, plane_rest, last_rest)
+                first_layer_pass(accs, j0, n, a, gw)
+            if j0 == 0:
+                load_scale_rows(nc.sync, w1s_rest, w1_scales[2:E])
+                nc.sync.dma_start(out=w2[:].bitcast(I32), in_=w2_words[:, 0].rearrange("e p b -> p e b").bitcast(I32))
+                load_scale_rows(nc.sync, w2s, w2_scales)
+            if j0 == 8:
+                nc.sync.dma_start(pos1_t[:], pos1)
+                nc.sync.dma_start(pos2_t[:], pos2)
+                gates = [w1_ring.tile([P, T], F32, name="w1", align_bytes=64) for r in range(2)]
+                for r in range(2):
+                    nc.sync.dma_start(out=gates[r][:], in_=gate[r])
+            hbs = [activate(j0 + i, accs[i]) for i in range(n)]
+            ht = held("ht%d" % j0, [P, n * H], BF16)
+            for i in range(0, n, 2):
+                turn(hbs[i : i + 2], ht[:, i * H : min(i + 2, n) * H])
+            hts.append(ht)
+
+        hw = held("xw%d" % (PASSES - 1), [P, S], U32)
+        hs = held("hs", [P, S], U8)
+        for (j0, n), ht in zip(CHUNKS, hts):
+            s0, s1 = j0 * P, (j0 + n) * P
+            nc.vector.quantize_mx(out=hw[:, s0:s1].bitcast(FP8X4), scales=hs[:, s0:s1], in_=ht[:])
+            y_ps = acc_pool.tile([P, n * P], F32, name="acc")
+            for c0 in range(s0, s1, C):
+                c1 = min(c0 + C, s1)
+                nc.tensor.matmul_mx(
+                    out=y_ps[:, c0 - s0 : c1 - s0],
+                    lhsT=w2[:, c0 // C, :].bitcast(FP4X4),
+                    lhsT_scale=w2s[:, c0 // C, :],
+                    rhs=hw[:, c0:c1].bitcast(FP8X4),
+                    rhs_scale=hs[:, c0:c1],
+                    start=True,
+                    stop=True,
+                )
+            if n == 4:
+                nc.scalar.copy(out=y[:, s0:s1], in_=y_ps[:])
+            else:
+                nc.vector.tensor_copy(out=y[:, s0:s1], in_=y_ps[:])
+
+        first = held("first", [P, T], F32)
+        nc.vector.tensor_tensor(first[:], y[:].indirect(pos1_t[:]), gates[0][:], MULT)
+        half = T // 2
+        for b in range(2):
+            cols = slice(b * half, (b + 1) * half)
+            second = held("second%d" % b, [P, half], F32)
+            res = held("res%d" % b, [P, half], F32)
+            nc.vector.tensor_tensor(
+                second[:], y[:].indirect(pos2_t[:, b * half // 16 : (b + 1) * half // 16]), gates[1][:, cols], MULT
+            )
+            nc.vector.tensor_tensor(res[:], first[:, cols], second[:], ADD)
+            nc.sync.dma_start(out=out[:, cols], in_=res[:])

@@ -21,8 +21,10 @@ GELU = mybir.ActivationFunctionType.Gelu_apprx_tanh
 MULT = mybir.AluOpType.mult
 ADD = mybir.AluOpType.add
 
-CHUNKS = [(0, 4), (4, 4), (8, 2), (10, 1), (11, 1)]
-HEAD = 512
+CHUNKS = [(0, 6), (6, 2), (8, 2), (10, 1), (11, 1)]
+HEAD = 768
+HEAD_E = HEAD // C
+GATHER = 384
 QUADS = (0, 2, 1, 3)
 
 
@@ -33,8 +35,7 @@ def tile_moe_pkd_mlp_gelu_kernel(
     with ExitStack() as ctx:
         lists = ctx.enter_context(tc.tile_pool(name="lists", bufs=1))
         keep = ctx.enter_context(tc.tile_pool(name="keep", bufs=1))
-        word_ring = ctx.enter_context(tc.tile_pool(name="word_ring", bufs=4))
-        w1_ring = ctx.enter_context(tc.tile_pool(name="w1_ring", bufs=7))
+        word_ring = ctx.enter_context(tc.tile_pool(name="word_ring", bufs=12))
         acc_pool = ctx.enter_context(tc.psum_pool(name="acc", bufs=6))
         turn_pool = ctx.enter_context(tc.psum_pool(name="turn", bufs=2))
 
@@ -47,14 +48,14 @@ def tile_moe_pkd_mlp_gelu_kernel(
 
         xs = held("xs", [P, T], U8)
         xw = [held("xw%d" % a, [P, T], I32) for a in range(PASSES)]
-        plane_head = held("plane_head", [P, 4, HEAD], U8)
-        plane_rest = held("plane_rest", [P, 4, S - HEAD], U8)
-        last_head = held("last_head", [P, HEAD], U8)
-        last_rest = held("last_rest", [P, S - HEAD], U8)
-        w1s_head = held("w1s_head", [P, 2 * PASSES, H], U8)
-        w1s_rest = held("w1s_rest", [P, 4 * PASSES, H], U8)
+        gs = held("gs", [P, S], U8)
+        plane_four = [held("plane_four%d" % b, [P, 4, HEAD], U8) for b in range(2)]
+        plane_last = held("plane_last", [P, S], U8)
+        w1s = [held("w1s%d" % b, [P, HEAD_E * PASSES, H], U8) for b in range(2)]
+        w1_head = [held("w1h%d" % a, [P, HEAD_E, 2 * H], U8) for a in range(PASSES)]
+        w1_rest = [held("w1r%d" % e, [P, PASSES, 2 * H], U8) for e in range(HEAD_E, E)]
+        gates = [held("gate%d" % r, [P, T], F32) for r in range(2)]
         w2s = held("w2s", [P, E, N], U8)
-        w1 = {}
         w2 = held("w2", [P, E, 2 * N], U8)
         ident = held("ident", [P, P], F32)
         y = held("y", [P, S], F32)
@@ -67,37 +68,22 @@ def tile_moe_pkd_mlp_gelu_kernel(
         def load_x(a):
             nc.sync.dma_start(out=xw[a][:], in_=x_words[a].rearrange("p t r -> p (t r)").bitcast(I32))
 
-        def load_w1(pair, a):
-            w1[pair, a] = w1_ring.tile([P, 2, 2 * H], U8, name="w1", align_bytes=64)
-            nc.sync.dma_start(
-                out=w1[pair, a][:].bitcast(I32),
-                in_=w1_words[2 * pair : 2 * pair + 2, a].rearrange("e p b -> p e b").bitcast(I32),
-            )
-
-        def gather_scales(s0, s1, four, last):
-            gs = keep.tile([P, s1 - s0], U8, name="gs", align_bytes=64)
-            for c in range(s0, s1, HEAD):
-                nc.vector.tensor_copy(
-                    gs[:, c - s0 : c - s0 + HEAD], xs[:].indirect(offs_t[:, c // 16 : (c + HEAD) // 16])
-                )
+        def move_four(queue, b):
             for q in QUADS:
-                nc.scalar.dma_start(
-                    out=four[32 * q : 32 * q + 4].bitcast(I32), in_=gs[16 * q : 16 * q + 16, :].bitcast(I32)
-                )
-            for q in QUADS:
-                nc.scalar.dma_start(
-                    out=last[32 * q : 32 * q + 4, :].bitcast(I32), in_=gs[112 + 4 * q : 116 + 4 * q, :].bitcast(I32)
+                queue.dma_start(
+                    out=plane_four[b][32 * q : 32 * q + 4].bitcast(I32),
+                    in_=gs[16 * q : 16 * q + 16, b * HEAD : (b + 1) * HEAD].bitcast(I32),
                 )
 
         def x_plane(a, j):
-            four, last, s0 = (plane_head, last_head, j * P) if j * P < HEAD else (plane_rest, last_rest, j * P - HEAD)
-            return last[:, s0 : s0 + P] if a == PASSES - 1 else four[:, a, s0 : s0 + P]
+            if a == PASSES - 1:
+                return plane_last[:, j * P : (j + 1) * P]
+            b, s0 = divmod(j * P, HEAD)
+            return plane_four[b][:, a, s0 : s0 + P]
 
         def w1_operand(e, a):
-            words = w1[e // 2, a][:, e % 2, :].bitcast(FP4X4)
-            if e < 2:
-                return words, w1s_head[:, e * PASSES + a, :]
-            return words, w1s_rest[:, (e - 2) * PASSES + a, :]
+            words = w1_head[a][:, e, :] if e < HEAD_E else w1_rest[e - HEAD_E][:, a, :]
+            return words.bitcast(FP4X4), w1s[e // HEAD_E][:, (e % HEAD_E) * PASSES + a, :]
 
         nc.vector.memset(xs[64:112, :].bitcast(I32), 0)
         make_identity(nc, ident[:])
@@ -107,14 +93,41 @@ def tile_moe_pkd_mlp_gelu_kernel(
             out=xs[0:64, :].bitcast(I32), in_=x_scales[0:4].rearrange("a f t -> f a t").bitcast(I32)
         )
         nc.scalar.dma_start(out=xs[112:P, :].bitcast(I32), in_=x_scales[4].bitcast(I32))
-        load_x(0)
-        load_scale_rows(nc.sync, w1s_head, w1_scales[0:2])
-        load_w1(0, 0)
-        gather_scales(0, HEAD, plane_head, last_head)
+        for c in range(0, S, GATHER):
+            nc.vector.tensor_copy(gs[:, c : c + GATHER], xs[:].indirect(offs_t[:, c // 16 : (c + GATHER) // 16]))
+        move_four(nc.scalar, 0)
+        for a in range(PASSES):
+            load_x(a)
+            if a == 0:
+                load_scale_rows(nc.sync, w1s[0], w1_scales[0:HEAD_E])
+            if a == PASSES - 1:
+                for q in QUADS:
+                    nc.sync.dma_start(
+                        out=plane_last[32 * q : 32 * q + 4, :].bitcast(I32),
+                        in_=gs[112 + 4 * q : 116 + 4 * q, :].bitcast(I32),
+                    )
+            nc.sync.dma_start(
+                out=w1_head[a][:].bitcast(I32), in_=w1_words[0:HEAD_E, a].rearrange("e p b -> p e b").bitcast(I32)
+            )
+        move_four(nc.sync, 1)
+        load_scale_rows(nc.sync, w1s[1], w1_scales[HEAD_E:E])
+        for e in range(HEAD_E, E):
+            nc.sync.dma_start(
+                out=w1_rest[e - HEAD_E][:].bitcast(I32), in_=w1_words[e].rearrange("s p b -> p s b").bitcast(I32)
+            )
+        nc.sync.dma_start(out=w2[:].bitcast(I32), in_=w2_words[:, 0].rearrange("e p b -> p e b").bitcast(I32))
+        load_scale_rows(nc.sync, w2s, w2_scales)
+        nc.sync.dma_start(pos1_t[:], pos1)
+        nc.sync.dma_start(pos2_t[:], pos2)
+        for r in range(2):
+            nc.sync.dma_start(out=gates[r][:], in_=gate[r])
 
         def gather_words(j0, n, a):
             gw = word_ring.tile([P, n * P], U32, name="gw", align_bytes=64)
-            nc.vector.tensor_copy(gw[:], xw[a][:].bitcast(U32).indirect(offs_t[:, 8 * j0 : 8 * (j0 + n)]))
+            for c in range(0, n * P, GATHER):
+                c1 = min(c + GATHER, n * P)
+                entries = offs_t[:, (j0 * P + c) // 16 : (j0 * P + c1) // 16]
+                nc.vector.tensor_copy(gw[:, c:c1], xw[a][:].bitcast(U32).indirect(entries))
             return gw
 
         def first_layer_pass(accs, j0, n, a, gw):
@@ -156,49 +169,30 @@ def tile_moe_pkd_mlp_gelu_kernel(
         for j0, n in CHUNKS:
             accs = [acc_pool.tile([P, H], F32, name="acc") for i in range(n)]
             for a in range(PASSES):
-                if j0 == 0 and a + 1 < PASSES:
-                    load_x(a + 1)
-                    load_w1(0, a + 1)
-                if j0 > 0 and j0 % 4 == 0:
-                    load_w1(j0 // 4, a)
-                gw = gather_words(j0, n, a)
-                if j0 == 0 and a == 1:
-                    gather_scales(HEAD, S, plane_rest, last_rest)
-                first_layer_pass(accs, j0, n, a, gw)
-            if j0 == 0:
-                load_scale_rows(nc.sync, w1s_rest, w1_scales[2:E])
-                nc.sync.dma_start(out=w2[:].bitcast(I32), in_=w2_words[:, 0].rearrange("e p b -> p e b").bitcast(I32))
-                load_scale_rows(nc.sync, w2s, w2_scales)
-            if j0 == 8:
-                nc.sync.dma_start(pos1_t[:], pos1)
-                nc.sync.dma_start(pos2_t[:], pos2)
-                gates = [w1_ring.tile([P, T], F32, name="w1", align_bytes=64) for r in range(2)]
-                for r in range(2):
-                    nc.sync.dma_start(out=gates[r][:], in_=gate[r])
+                first_layer_pass(accs, j0, n, a, gather_words(j0, n, a))
             hbs = [activate(j0 + i, accs[i]) for i in range(n)]
-            ht = held("ht%d" % j0, [P, n * H], BF16)
             for i in range(0, n, 2):
-                turn(hbs[i : i + 2], ht[:, i * H : min(i + 2, n) * H])
-            hts.append(ht)
+                group = hbs[i : i + 2]
+                ht = held("ht%d" % (j0 + i), [P, len(group) * H], BF16)
+                turn(group, ht[:])
+                hts.append((j0 + i, len(group), ht))
 
         hw = held("xw%d" % (PASSES - 1), [P, S], U32)
         hs = held("hs", [P, S], U8)
-        for (j0, n), ht in zip(CHUNKS, hts):
+        for j0, n, ht in hts:
             s0, s1 = j0 * P, (j0 + n) * P
             nc.vector.quantize_mx(out=hw[:, s0:s1].bitcast(FP8X4), scales=hs[:, s0:s1], in_=ht[:])
             y_ps = acc_pool.tile([P, n * P], F32, name="acc")
-            for c0 in range(s0, s1, C):
-                c1 = min(c0 + C, s1)
-                nc.tensor.matmul_mx(
-                    out=y_ps[:, c0 - s0 : c1 - s0],
-                    lhsT=w2[:, c0 // C, :].bitcast(FP4X4),
-                    lhsT_scale=w2s[:, c0 // C, :],
-                    rhs=hw[:, c0:c1].bitcast(FP8X4),
-                    rhs_scale=hs[:, c0:c1],
-                    start=True,
-                    stop=True,
-                )
-            if n == 4:
+            nc.tensor.matmul_mx(
+                out=y_ps[:],
+                lhsT=w2[:, s0 // C, :].bitcast(FP4X4),
+                lhsT_scale=w2s[:, s0 // C, :],
+                rhs=hw[:, s0:s1].bitcast(FP8X4),
+                rhs_scale=hs[:, s0:s1],
+                start=True,
+                stop=True,
+            )
+            if j0 < 8:
                 nc.scalar.copy(out=y[:, s0:s1], in_=y_ps[:])
             else:
                 nc.vector.tensor_copy(out=y[:, s0:s1], in_=y_ps[:])

@@ -51,7 +51,7 @@ def tile_moe_pkd_mlp_gelu_kernel(
         gs = held("gs", [P, S], U8)
         plane_four = [held("plane_four%d" % b, [P, 4, HEAD], U8) for b in range(2)]
         plane_last = held("plane_last", [P, S], U8)
-        w1s = [held("w1s%d" % b, [P, HEAD_E * PASSES, H], U8) for b in range(2)]
+        w1s = held("w1s", [P, E * PASSES, H], U8)
         w1_head = [held("w1h%d" % a, [P, HEAD_E, 2 * H], U8) for a in range(PASSES)]
         w1_rest = [held("w1r%d" % e, [P, PASSES, 2 * H], U8) for e in range(HEAD_E, E)]
         gates = [held("gate%d" % r, [P, T], F32) for r in range(2)]
@@ -83,7 +83,7 @@ def tile_moe_pkd_mlp_gelu_kernel(
 
         def w1_operand(e, a):
             words = w1_head[a][:, e, :] if e < HEAD_E else w1_rest[e - HEAD_E][:, a, :]
-            return words.bitcast(FP4X4), w1s[e // HEAD_E][:, (e % HEAD_E) * PASSES + a, :]
+            return words.bitcast(FP4X4), w1s[:, e * PASSES + a, :]
 
         nc.vector.memset(xs[64:112, :].bitcast(I32), 0)
         make_identity(nc, ident[:])
@@ -95,22 +95,27 @@ def tile_moe_pkd_mlp_gelu_kernel(
         nc.scalar.dma_start(out=xs[112:P, :].bitcast(I32), in_=x_scales[4].bitcast(I32))
         for c in range(0, S, GATHER):
             nc.vector.tensor_copy(gs[:, c : c + GATHER], xs[:].indirect(offs_t[:, c // 16 : (c + GATHER) // 16]))
-        move_four(nc.scalar, 0)
-        for a in range(PASSES):
-            load_x(a)
-            if a == 0:
-                load_scale_rows(nc.sync, w1s[0], w1_scales[0:HEAD_E])
-            if a == PASSES - 1:
-                for q in QUADS:
-                    nc.sync.dma_start(
-                        out=plane_last[32 * q : 32 * q + 4, :].bitcast(I32),
-                        in_=gs[112 + 4 * q : 116 + 4 * q, :].bitcast(I32),
-                    )
+
+        def load_w1_head(a):
             nc.sync.dma_start(
                 out=w1_head[a][:].bitcast(I32), in_=w1_words[0:HEAD_E, a].rearrange("e p b -> p e b").bitcast(I32)
             )
+
+        load_scale_rows(nc.sync, w1s, w1_scales)
+        load_x(0)
+        load_w1_head(0)
+        move_four(nc.sync, 0)
         move_four(nc.sync, 1)
-        load_scale_rows(nc.sync, w1s[1], w1_scales[HEAD_E:E])
+        for q in QUADS:
+            nc.sync.dma_start(
+                out=plane_last[32 * q : 32 * q + 4, :].bitcast(I32),
+                in_=gs[112 + 4 * q : 116 + 4 * q, :].bitcast(I32),
+            )
+        load_x(1)
+        for a in range(1, PASSES):
+            if a + 1 < PASSES:
+                load_x(a + 1)
+            load_w1_head(a)
         for e in range(HEAD_E, E):
             nc.sync.dma_start(
                 out=w1_rest[e - HEAD_E][:].bitcast(I32), in_=w1_words[e].rearrange("s p b -> p s b").bitcast(I32)
@@ -170,9 +175,8 @@ def tile_moe_pkd_mlp_gelu_kernel(
             accs = [acc_pool.tile([P, H], F32, name="acc") for i in range(n)]
             for a in range(PASSES):
                 first_layer_pass(accs, j0, n, a, gather_words(j0, n, a))
-            hbs = [activate(j0 + i, accs[i]) for i in range(n)]
             for i in range(0, n, 2):
-                group = hbs[i : i + 2]
+                group = [activate(j0 + k, accs[k]) for k in range(i, min(i + 2, n))]
                 ht = held("ht%d" % (j0 + i), [P, len(group) * H], BF16)
                 turn(group, ht[:])
                 hts.append((j0 + i, len(group), ht))
@@ -199,13 +203,9 @@ def tile_moe_pkd_mlp_gelu_kernel(
 
         first = held("first", [P, T], F32)
         nc.vector.tensor_tensor(first[:], y[:].indirect(pos1_t[:]), gates[0][:], MULT)
-        half = T // 2
-        for b in range(2):
-            cols = slice(b * half, (b + 1) * half)
-            second = held("second%d" % b, [P, half], F32)
-            res = held("res%d" % b, [P, half], F32)
-            nc.vector.tensor_tensor(
-                second[:], y[:].indirect(pos2_t[:, b * half // 16 : (b + 1) * half // 16]), gates[1][:, cols], MULT
-            )
-            nc.vector.tensor_tensor(res[:], first[:, cols], second[:], ADD)
-            nc.sync.dma_start(out=out[:, cols], in_=res[:])
+        for t0, t1 in ((0, 512), (512, T)):
+            second = held("second%d" % t0, [P, t1 - t0], F32)
+            res = held("res%d" % t0, [P, t1 - t0], F32)
+            nc.vector.tensor_tensor(second[:], y[:].indirect(pos2_t[:, t0 // 16 : t1 // 16]), gates[1][:, t0:t1], MULT)
+            nc.vector.tensor_tensor(res[:], first[:, t0:t1], second[:], ADD)
+            nc.sync.dma_start(out=out[:, t0:t1], in_=res[:])

@@ -25,6 +25,7 @@ CHUNKS = [(0, 6), (6, 2), (8, 2), (10, 1), (11, 1)]
 HEAD = 768
 HEAD_E = HEAD // C
 GATHER = 384
+SCALE_SETS = ((0, HEAD_E), (HEAD_E, E))
 QUADS = (0, 2, 1, 3)
 
 
@@ -51,7 +52,7 @@ def tile_moe_pkd_mlp_gelu_kernel(
         gs = held("gs", [P, S], U8)
         plane_four = [held("plane_four%d" % b, [P, 4, HEAD], U8) for b in range(2)]
         plane_last = held("plane_last", [P, S], U8)
-        w1s = held("w1s", [P, E * PASSES, H], U8)
+        w1s = [held("w1s%d" % e0, [P, (e1 - e0) * PASSES, H], U8) for e0, e1 in SCALE_SETS]
         w1_head = [held("w1h%d" % a, [P, HEAD_E, 2 * H], U8) for a in range(PASSES)]
         w1_rest = [held("w1r%d" % e, [P, PASSES, 2 * H], U8) for e in range(HEAD_E, E)]
         gates = [held("gate%d" % r, [P, T], F32) for r in range(2)]
@@ -60,9 +61,9 @@ def tile_moe_pkd_mlp_gelu_kernel(
         ident = held("ident", [P, P], F32)
         y = held("y", [P, S], F32)
 
-        def load_scale_rows(queue, dst, src):
+        def load_scale_rows(queue, dst, src, which=range(4)):
             rows = src.rearrange("e s (q r) n -> r q (e s) n", r=4)
-            for r in range(4):
+            for r in which:
                 queue.dma_start(out=dst[r:P:32].bitcast(I32), in_=rows[r].bitcast(I32))
 
         def load_x(a):
@@ -83,9 +84,11 @@ def tile_moe_pkd_mlp_gelu_kernel(
 
         def w1_operand(e, a):
             words = w1_head[a][:, e, :] if e < HEAD_E else w1_rest[e - HEAD_E][:, a, :]
-            return words.bitcast(FP4X4), w1s[:, e * PASSES + a, :]
+            b = [e0 <= e < e1 for e0, e1 in SCALE_SETS].index(True)
+            return words.bitcast(FP4X4), w1s[b][:, (e - SCALE_SETS[b][0]) * PASSES + a, :]
 
         nc.vector.memset(xs[64:112, :].bitcast(I32), 0)
+        load_scale_rows(nc.gpsimd, w1s[0], w1_scales[0:HEAD_E], range(2))
         make_identity(nc, ident[:])
 
         nc.sync.dma_start(offs_t[:], offs)
@@ -101,25 +104,28 @@ def tile_moe_pkd_mlp_gelu_kernel(
                 out=w1_head[a][:].bitcast(I32), in_=w1_words[0:HEAD_E, a].rearrange("e p b -> p e b").bitcast(I32)
             )
 
-        load_scale_rows(nc.sync, w1s, w1_scales)
+        move_four(nc.scalar, 0)
         load_x(0)
+        load_scale_rows(nc.sync, w1s[0], w1_scales[0:HEAD_E], range(2, 4))
         load_w1_head(0)
-        move_four(nc.sync, 0)
-        move_four(nc.sync, 1)
-        for q in QUADS:
-            nc.sync.dma_start(
-                out=plane_last[32 * q : 32 * q + 4, :].bitcast(I32),
-                in_=gs[112 + 4 * q : 116 + 4 * q, :].bitcast(I32),
-            )
         load_x(1)
         for a in range(1, PASSES):
             if a + 1 < PASSES:
                 load_x(a + 1)
+            else:
+                for q in QUADS:
+                    nc.sync.dma_start(
+                        out=plane_last[32 * q : 32 * q + 4, :].bitcast(I32),
+                        in_=gs[112 + 4 * q : 116 + 4 * q, :].bitcast(I32),
+                    )
             load_w1_head(a)
-        for e in range(HEAD_E, E):
-            nc.sync.dma_start(
-                out=w1_rest[e - HEAD_E][:].bitcast(I32), in_=w1_words[e].rearrange("s p b -> p s b").bitcast(I32)
-            )
+        move_four(nc.sync, 1)
+        for (e0, e1), plane in zip(SCALE_SETS[1:], w1s[1:]):
+            load_scale_rows(nc.sync, plane, w1_scales[e0:e1])
+            for e in range(e0, e1):
+                nc.sync.dma_start(
+                    out=w1_rest[e - HEAD_E][:].bitcast(I32), in_=w1_words[e].rearrange("s p b -> p s b").bitcast(I32)
+                )
         nc.sync.dma_start(out=w2[:].bitcast(I32), in_=w2_words[:, 0].rearrange("e p b -> p e b").bitcast(I32))
         load_scale_rows(nc.sync, w2s, w2_scales)
         nc.sync.dma_start(pos1_t[:], pos1)
@@ -149,13 +155,15 @@ def tile_moe_pkd_mlp_gelu_kernel(
                     stop=(a == PASSES - 1),
                 )
 
-        def activate(j, acc):
+        def activate(j, acc, pieces):
             hb = held("hb%d" % j, [P, H], BF16)
-            nc.scalar.activation(
-                out=hb[:].rearrange("s (u p e) -> s u p e", u=2, e=2),
-                in_=acc[:].rearrange("s (p u e) -> s u p e", u=2, e=2),
-                func=GELU,
-            )
+            step = 2 // pieces
+            for u in range(0, 2, step):
+                nc.scalar.activation(
+                    out=hb[:].rearrange("s (u p e) -> s u p e", u=2, e=2)[:, u : u + step],
+                    in_=acc[:].rearrange("s (p u e) -> s u p e", u=2, e=2)[:, u : u + step],
+                    func=GELU,
+                )
             return hb
 
         def turn(hbs, ht):
@@ -175,8 +183,9 @@ def tile_moe_pkd_mlp_gelu_kernel(
             accs = [acc_pool.tile([P, H], F32, name="acc") for i in range(n)]
             for a in range(PASSES):
                 first_layer_pass(accs, j0, n, a, gather_words(j0, n, a))
+            hbs = [activate(j0 + k, accs[k], 1) for k in range(n)]
             for i in range(0, n, 2):
-                group = [activate(j0 + k, accs[k]) for k in range(i, min(i + 2, n))]
+                group = hbs[i : i + 2]
                 ht = held("ht%d" % (j0 + i), [P, len(group) * H], BF16)
                 turn(group, ht[:])
                 hts.append((j0 + i, len(group), ht))
@@ -203,7 +212,7 @@ def tile_moe_pkd_mlp_gelu_kernel(
 
         first = held("first", [P, T], F32)
         nc.vector.tensor_tensor(first[:], y[:].indirect(pos1_t[:]), gates[0][:], MULT)
-        for t0, t1 in ((0, 512), (512, T)):
+        for t0, t1 in ((0, T // 2), (T // 2, T)):
             second = held("second%d" % t0, [P, t1 - t0], F32)
             res = held("res%d" % t0, [P, t1 - t0], F32)
             nc.vector.tensor_tensor(second[:], y[:].indirect(pos2_t[:, t0 // 16 : t1 // 16]), gates[1][:, t0:t1], MULT)

@@ -21,12 +21,17 @@ GELU = mybir.ActivationFunctionType.Gelu_apprx_tanh
 MULT = mybir.AluOpType.mult
 ADD = mybir.AluOpType.add
 
-CHUNKS = [(0, 6), (6, 2), (8, 2), (10, 1), (11, 1)]
-HEAD = 768
-HEAD_E = HEAD // C
-GATHER = 384
-SCALE_SETS = ((0, HEAD_E), (HEAD_E, E))
+ALIGN = 256
+ACC_BANKS = 6
+TURN_BANKS = 2
+HEAD_EXPERTS = ACC_BANKS * P // C
+HEAD = HEAD_EXPERTS * C
+CHUNKS = [(0, ACC_BANKS), (6, 2), (8, 2), (10, 1), (11, 1)]
+LAST_TILE = S // P - 1
+GATHER = T // 2
+WORD_BUFS = 12
 QUADS = (0, 2, 1, 3)
+LAST_ROWS = P - 16
 
 
 def tile_moe_pkd_mlp_gelu_kernel(
@@ -36,185 +41,188 @@ def tile_moe_pkd_mlp_gelu_kernel(
     with ExitStack() as ctx:
         lists = ctx.enter_context(tc.tile_pool(name="lists", bufs=1))
         keep = ctx.enter_context(tc.tile_pool(name="keep", bufs=1))
-        word_ring = ctx.enter_context(tc.tile_pool(name="word_ring", bufs=12))
-        acc_pool = ctx.enter_context(tc.psum_pool(name="acc", bufs=6))
-        turn_pool = ctx.enter_context(tc.psum_pool(name="turn", bufs=2))
+        word_ring = ctx.enter_context(tc.tile_pool(name="word_ring", bufs=WORD_BUFS))
+        acc_pool = ctx.enter_context(tc.psum_pool(name="acc", bufs=ACC_BANKS))
+        turn_pool = ctx.enter_context(tc.psum_pool(name="turn", bufs=TURN_BANKS))
 
         def held(name, shape, dtype):
-            return keep.tile(shape, dtype, name=name, align_bytes=64)
+            return keep.tile(shape, dtype, name=name, align_bytes=ALIGN)
 
         offs_t = lists.tile([P, S // 16], U16, name="offs_t")
         pos1_t = lists.tile([P, T // 16], U16, name="pos1_t")
         pos2_t = lists.tile([P, T // 16], U16, name="pos2_t")
 
-        xs = held("xs", [P, T], U8)
-        xw = [held("xw%d" % a, [P, T], I32) for a in range(PASSES)]
-        gs = held("gs", [P, S], U8)
-        plane_four = [held("plane_four%d" % b, [P, 4, HEAD], U8) for b in range(2)]
-        plane_last = held("plane_last", [P, S], U8)
-        w1s = [held("w1s%d" % e0, [P, (e1 - e0) * PASSES, H], U8) for e0, e1 in SCALE_SETS]
-        w1_head = [held("w1h%d" % a, [P, HEAD_E, 2 * H], U8) for a in range(PASSES)]
-        w1_rest = [held("w1r%d" % e, [P, PASSES, 2 * H], U8) for e in range(HEAD_E, E)]
+        scale_window = held("scale_window", [P, T], U8)
+        word_windows = [held("word_window%d" % a, [P, T], I32) for a in range(PASSES)]
+        slot_scales = held("slot_scales", [P, S], U8)
+        first_planes = [held("first_planes%d" % b, [P, 4, HEAD], U8) for b in range(2)]
+        last_plane = held("last_plane", [P, S], U8)
+        w1_planes = [held("w1_planes%d" % b, [P, HEAD_EXPERTS * PASSES, H], U8) for b in range(2)]
+        w1_head = [held("w1_head%d" % a, [P, HEAD_EXPERTS, 2 * H], U8) for a in range(PASSES)]
+        w1_rest = [held("w1_rest%d" % e, [P, PASSES, 2 * H], U8) for e in range(HEAD_EXPERTS, E)]
         gates = [held("gate%d" % r, [P, T], F32) for r in range(2)]
-        w2s = held("w2s", [P, E, N], U8)
+        w2_planes = held("w2_planes", [P, E, N], U8)
         w2 = held("w2", [P, E, 2 * N], U8)
         ident = held("ident", [P, P], F32)
         y = held("y", [P, S], F32)
 
-        def load_scale_rows(queue, dst, src, which=range(4)):
-            rows = src.rearrange("e s (q r) n -> r q (e s) n", r=4)
-            for r in which:
-                queue.dma_start(out=dst[r:P:32].bitcast(I32), in_=rows[r].bitcast(I32))
+        def load_weight_planes(planes, scales):
+            rows = scales.rearrange("e s (q r) n -> r q (e s) n", r=4)
+            for r in range(4):
+                nc.sync.dma_start(out=planes[r:P:32].bitcast(I32), in_=rows[r].bitcast(I32))
 
         def load_x(a):
-            nc.sync.dma_start(out=xw[a][:], in_=x_words[a].rearrange("p t r -> p (t r)").bitcast(I32))
+            nc.sync.dma_start(out=word_windows[a][:], in_=x_words[a].rearrange("p t r -> p (t r)").bitcast(I32))
 
-        def move_four(queue, b):
+        def load_w1_head(a):
+            words = w1_words[0:HEAD_EXPERTS, a].rearrange("e p b -> p e b")
+            nc.sync.dma_start(out=w1_head[a][:].bitcast(I32), in_=words.bitcast(I32))
+
+        def move_first_planes(queue, b):
             for q in QUADS:
                 queue.dma_start(
-                    out=plane_four[b][32 * q : 32 * q + 4].bitcast(I32),
-                    in_=gs[16 * q : 16 * q + 16, b * HEAD : (b + 1) * HEAD].bitcast(I32),
+                    out=first_planes[b][32 * q : 32 * q + 4].bitcast(I32),
+                    in_=slot_scales[16 * q : 16 * q + 16, b * HEAD : (b + 1) * HEAD].bitcast(I32),
                 )
 
-        def x_plane(a, j):
+        def move_last_plane():
+            for q in QUADS:
+                nc.sync.dma_start(
+                    out=last_plane[32 * q : 32 * q + 4, :].bitcast(I32),
+                    in_=slot_scales[LAST_ROWS + 4 * q : LAST_ROWS + 4 * q + 4, :].bitcast(I32),
+                )
+
+        def token_plane(a, j):
             if a == PASSES - 1:
-                return plane_last[:, j * P : (j + 1) * P]
+                return last_plane[:, j * P : (j + 1) * P]
             b, s0 = divmod(j * P, HEAD)
-            return plane_four[b][:, a, s0 : s0 + P]
+            return first_planes[b][:, a, s0 : s0 + P]
 
         def w1_operand(e, a):
-            words = w1_head[a][:, e, :] if e < HEAD_E else w1_rest[e - HEAD_E][:, a, :]
-            b = [e0 <= e < e1 for e0, e1 in SCALE_SETS].index(True)
-            return words.bitcast(FP4X4), w1s[b][:, (e - SCALE_SETS[b][0]) * PASSES + a, :]
+            b, within = divmod(e, HEAD_EXPERTS)
+            words = w1_head[a][:, e, :] if b == 0 else w1_rest[within][:, a, :]
+            return words.bitcast(FP4X4), w1_planes[b][:, within * PASSES + a, :]
 
-        nc.vector.memset(xs[64:112, :].bitcast(I32), 0)
-        load_scale_rows(nc.gpsimd, w1s[0], w1_scales[0:HEAD_E], range(2))
+        nc.vector.memset(scale_window[64:LAST_ROWS, :].bitcast(I32), 0)
         make_identity(nc, ident[:])
 
         nc.sync.dma_start(offs_t[:], offs)
         nc.scalar.dma_start(
-            out=xs[0:64, :].bitcast(I32), in_=x_scales[0:4].rearrange("a f t -> f a t").bitcast(I32)
+            out=scale_window[0:64, :].bitcast(I32), in_=x_scales[0:4].rearrange("a f t -> f a t").bitcast(I32)
         )
-        nc.scalar.dma_start(out=xs[112:P, :].bitcast(I32), in_=x_scales[4].bitcast(I32))
+        nc.scalar.dma_start(out=scale_window[LAST_ROWS:P, :].bitcast(I32), in_=x_scales[PASSES - 1].bitcast(I32))
         for c in range(0, S, GATHER):
-            nc.vector.tensor_copy(gs[:, c : c + GATHER], xs[:].indirect(offs_t[:, c // 16 : (c + GATHER) // 16]))
+            entries = offs_t[:, c // 16 : (c + GATHER) // 16]
+            nc.vector.tensor_copy(slot_scales[:, c : c + GATHER], scale_window[:].indirect(entries))
 
-        def load_w1_head(a):
-            nc.sync.dma_start(
-                out=w1_head[a][:].bitcast(I32), in_=w1_words[0:HEAD_E, a].rearrange("e p b -> p e b").bitcast(I32)
-            )
-
-        move_four(nc.scalar, 0)
+        move_first_planes(nc.scalar, 0)
         load_x(0)
-        load_scale_rows(nc.sync, w1s[0], w1_scales[0:HEAD_E], range(2, 4))
+        load_weight_planes(w1_planes[0], w1_scales[0:HEAD_EXPERTS])
         load_w1_head(0)
         load_x(1)
         for a in range(1, PASSES):
             if a + 1 < PASSES:
                 load_x(a + 1)
             else:
-                for q in QUADS:
-                    nc.sync.dma_start(
-                        out=plane_last[32 * q : 32 * q + 4, :].bitcast(I32),
-                        in_=gs[112 + 4 * q : 116 + 4 * q, :].bitcast(I32),
-                    )
+                move_last_plane()
             load_w1_head(a)
-        move_four(nc.sync, 1)
-        for (e0, e1), plane in zip(SCALE_SETS[1:], w1s[1:]):
-            load_scale_rows(nc.sync, plane, w1_scales[e0:e1])
-            for e in range(e0, e1):
-                nc.sync.dma_start(
-                    out=w1_rest[e - HEAD_E][:].bitcast(I32), in_=w1_words[e].rearrange("s p b -> p s b").bitcast(I32)
-                )
+        move_first_planes(nc.sync, 1)
+        load_weight_planes(w1_planes[1], w1_scales[HEAD_EXPERTS:E])
+        for e in range(HEAD_EXPERTS, E):
+            words = w1_words[e].rearrange("s p b -> p s b")
+            nc.sync.dma_start(out=w1_rest[e - HEAD_EXPERTS][:].bitcast(I32), in_=words.bitcast(I32))
         nc.sync.dma_start(out=w2[:].bitcast(I32), in_=w2_words[:, 0].rearrange("e p b -> p e b").bitcast(I32))
-        load_scale_rows(nc.sync, w2s, w2_scales)
+        load_weight_planes(w2_planes, w2_scales)
         nc.sync.dma_start(pos1_t[:], pos1)
         nc.sync.dma_start(pos2_t[:], pos2)
         for r in range(2):
             nc.sync.dma_start(out=gates[r][:], in_=gate[r])
 
         def gather_words(j0, n, a):
-            gw = word_ring.tile([P, n * P], U32, name="gw", align_bytes=64)
-            for c in range(0, n * P, GATHER):
-                c1 = min(c + GATHER, n * P)
-                entries = offs_t[:, (j0 * P + c) // 16 : (j0 * P + c1) // 16]
-                nc.vector.tensor_copy(gw[:, c:c1], xw[a][:].bitcast(U32).indirect(entries))
-            return gw
+            slot_words = word_ring.tile([P, n * P], U32, name="slot_words", align_bytes=ALIGN)
+            for c0 in range(0, n * P, GATHER):
+                c1 = min(c0 + GATHER, n * P)
+                entries = offs_t[:, (j0 * P + c0) // 16 : (j0 * P + c1) // 16]
+                nc.vector.tensor_copy(slot_words[:, c0:c1], word_windows[a][:].bitcast(U32).indirect(entries))
+            return slot_words
 
-        def first_layer_pass(accs, j0, n, a, gw):
-            for i in range(n):
+        def first_layer_pass(accs, j0, a, slot_words):
+            for i, acc in enumerate(accs):
                 j = j0 + i
-                w, ws = w1_operand(j // 2, a)
+                w1_codes, w1_plane = w1_operand(j * P // C, a)
                 nc.tensor.matmul_mx(
-                    out=accs[i][:],
-                    lhsT=gw[:, i * P : (i + 1) * P].bitcast(FP8X4),
-                    lhsT_scale=x_plane(a, j),
-                    rhs=w,
-                    rhs_scale=ws,
+                    out=acc[:],
+                    lhsT=slot_words[:, i * P : (i + 1) * P].bitcast(FP8X4),
+                    lhsT_scale=token_plane(a, j),
+                    rhs=w1_codes,
+                    rhs_scale=w1_plane,
                     start=(a == 0),
                     stop=(a == PASSES - 1),
                 )
 
-        def activate(j, acc, pieces):
-            hb = held("hb%d" % j, [P, H], BF16)
-            step = 2 // pieces
+        def activate(j, acc):
+            h = held("h%d" % j, [P, H], BF16)
+            step = 1 if j == LAST_TILE else 2
             for u in range(0, 2, step):
                 nc.scalar.activation(
-                    out=hb[:].rearrange("s (u p e) -> s u p e", u=2, e=2)[:, u : u + step],
-                    in_=acc[:].rearrange("s (p u e) -> s u p e", u=2, e=2)[:, u : u + step],
+                    out=h[:].rearrange("s (u p d) -> s u p d", u=2, d=2)[:, u : u + step],
+                    in_=acc[:].rearrange("s (p u d) -> s u p d", u=2, d=2)[:, u : u + step],
                     func=GELU,
                 )
-            return hb
+            return h
 
-        def turn(hbs, ht):
-            n = len(hbs)
-            turned = turn_pool.tile([P, n, 2, P], F32, name="turned")
-            for i in range(n):
-                words = hbs[i][:].bitcast(F32)
-                for u in range(2):
-                    nc.tensor.transpose(turned[:, i, u, :], words[:, u * P : (u + 1) * P], ident[:])
-            nc.scalar.copy(
-                out=ht.bitcast(F32).rearrange("p (i s u) -> p i s u", i=n, u=2),
-                in_=turned[:].rearrange("p i u s -> p i s u"),
-            )
+        turned_groups = []
 
-        hts = []
+        def turn_groups(groups):
+            for j, group in groups:
+                n = len(group)
+                h_turned = held("h_turned%d" % j, [P, n * H], BF16)
+                bank = turn_pool.tile([P, n, 2, P], F32, name="bank")
+                for i, h in enumerate(group):
+                    pairs = h[:].bitcast(F32)
+                    for u in range(2):
+                        nc.tensor.transpose(bank[:, i, u, :], pairs[:, u * P : (u + 1) * P], ident[:])
+                nc.scalar.copy(
+                    out=h_turned[:].bitcast(F32).rearrange("p (i s u) -> p i s u", i=n, u=2),
+                    in_=bank[:].rearrange("p i u s -> p i s u"),
+                )
+                turned_groups.append((j, n, h_turned))
+
+        waiting = []
         for j0, n in CHUNKS:
             accs = [acc_pool.tile([P, H], F32, name="acc") for i in range(n)]
             for a in range(PASSES):
-                first_layer_pass(accs, j0, n, a, gather_words(j0, n, a))
-            hbs = [activate(j0 + k, accs[k], 1) for k in range(n)]
-            for i in range(0, n, 2):
-                group = hbs[i : i + 2]
-                ht = held("ht%d" % (j0 + i), [P, len(group) * H], BF16)
-                turn(group, ht[:])
-                hts.append((j0 + i, len(group), ht))
+                first_layer_pass(accs, j0, a, gather_words(j0, n, a))
+            h_tiles = [activate(j0 + i, acc) for i, acc in enumerate(accs)]
+            turn_groups(waiting)
+            waiting = [(j0 + i, h_tiles[i : i + 2]) for i in range(0, n, 2)]
+        turn_groups(waiting)
 
-        hw = held("xw%d" % (PASSES - 1), [P, S], U32)
-        hs = held("hs", [P, S], U8)
-        for j0, n, ht in hts:
-            s0, s1 = j0 * P, (j0 + n) * P
-            nc.vector.quantize_mx(out=hw[:, s0:s1].bitcast(FP8X4), scales=hs[:, s0:s1], in_=ht[:])
-            y_ps = acc_pool.tile([P, n * P], F32, name="acc")
+        h_words = held("word_window%d" % (PASSES - 1), [P, S], U32)
+        h_plane = held("h_plane", [P, S], U8)
+        for j, n, h_turned in turned_groups:
+            s0, s1 = j * P, (j + n) * P
+            nc.vector.quantize_mx(out=h_words[:, s0:s1].bitcast(FP8X4), scales=h_plane[:, s0:s1], in_=h_turned[:])
+            y_bank = acc_pool.tile([P, n * P], F32, name="acc")
             nc.tensor.matmul_mx(
-                out=y_ps[:],
+                out=y_bank[:],
                 lhsT=w2[:, s0 // C, :].bitcast(FP4X4),
-                lhsT_scale=w2s[:, s0 // C, :],
-                rhs=hw[:, s0:s1].bitcast(FP8X4),
-                rhs_scale=hs[:, s0:s1],
+                lhsT_scale=w2_planes[:, s0 // C, :],
+                rhs=h_words[:, s0:s1].bitcast(FP8X4),
+                rhs_scale=h_plane[:, s0:s1],
                 start=True,
                 stop=True,
             )
-            if j0 < 8:
-                nc.scalar.copy(out=y[:, s0:s1], in_=y_ps[:])
+            if s0 // C < E - 2:
+                nc.scalar.copy(out=y[:, s0:s1], in_=y_bank[:])
             else:
-                nc.vector.tensor_copy(out=y[:, s0:s1], in_=y_ps[:])
+                nc.vector.tensor_copy(out=y[:, s0:s1], in_=y_bank[:])
 
         first = held("first", [P, T], F32)
         nc.vector.tensor_tensor(first[:], y[:].indirect(pos1_t[:]), gates[0][:], MULT)
         for t0, t1 in ((0, T // 2), (T // 2, T)):
             second = held("second%d" % t0, [P, t1 - t0], F32)
-            res = held("res%d" % t0, [P, t1 - t0], F32)
+            total = held("total%d" % t0, [P, t1 - t0], F32)
             nc.vector.tensor_tensor(second[:], y[:].indirect(pos2_t[:, t0 // 16 : t1 // 16]), gates[1][:, t0:t1], MULT)
-            nc.vector.tensor_tensor(res[:], first[:, t0:t1], second[:], ADD)
-            nc.sync.dma_start(out=out[:, t0:t1], in_=res[:])
+            nc.vector.tensor_tensor(total[:], first[:, t0:t1], second[:], ADD)
+            nc.sync.dma_start(out=out[:, t0:t1], in_=total[:])

@@ -22,16 +22,18 @@ MULT = mybir.AluOpType.mult
 ADD = mybir.AluOpType.add
 
 ALIGN = 256
-ACC_BANKS = 6
-TURN_BANKS = 2
-HEAD_EXPERTS = ACC_BANKS * P // C
-HEAD = HEAD_EXPERTS * C
-CHUNKS = [(0, ACC_BANKS), (6, 2), (8, 2), (10, 1), (11, 1)]
-LAST_TILE = S // P - 1
-GATHER = T // 2
+PAIR = 2
+HEAD = PAIR * C
+TILES = C // P
 WORD_BUFS = 12
+X_CUTS = ((0, 1), (1, 3), (3, PASSES))
+W1_CUTS = ((0, PASSES),)
 QUADS = (0, 2, 1, 3)
 LAST_ROWS = P - 16
+
+
+def cut_of(cuts, a):
+    return max(a0 for a0, a1 in cuts if a0 <= a)
 
 
 def tile_moe_pkd_mlp_gelu_kernel(
@@ -42,66 +44,101 @@ def tile_moe_pkd_mlp_gelu_kernel(
         lists = ctx.enter_context(tc.tile_pool(name="lists", bufs=1))
         keep = ctx.enter_context(tc.tile_pool(name="keep", bufs=1))
         word_ring = ctx.enter_context(tc.tile_pool(name="word_ring", bufs=WORD_BUFS))
-        acc_pool = ctx.enter_context(tc.psum_pool(name="acc", bufs=ACC_BANKS))
-        turn_pool = ctx.enter_context(tc.psum_pool(name="turn", bufs=TURN_BANKS))
+        banks = ctx.enter_context(tc.psum_pool(name="banks", bufs=1))
 
         def held(name, shape, dtype):
             return keep.tile(shape, dtype, name=name, align_bytes=ALIGN)
+
+        def bank_tile(b, shape):
+            return banks.tile(shape, F32, name="bank%d" % b)
 
         offs_t = lists.tile([P, S // 16], U16, name="offs_t")
         pos1_t = lists.tile([P, T // 16], U16, name="pos1_t")
         pos2_t = lists.tile([P, T // 16], U16, name="pos2_t")
 
         scale_window = held("scale_window", [P, T], U8)
-        word_windows = [held("word_window%d" % a, [P, T], I32) for a in range(PASSES)]
+        word_windows = {a0: held("word_window%d" % a0, [P, a1 - a0, T], I32) for a0, a1 in X_CUTS}
         slot_scales = held("slot_scales", [P, S], U8)
-        first_planes = [held("first_planes%d" % b, [P, 4, HEAD], U8) for b in range(2)]
+        head_planes = held("head_planes", [P, 4, HEAD], U8)
+        rest_planes = held("rest_planes", [P, 4, S - HEAD], U8)
         last_plane = held("last_plane", [P, S], U8)
-        w1_planes = [held("w1_planes%d" % b, [P, HEAD_EXPERTS * PASSES, H], U8) for b in range(2)]
-        w1_head = [held("w1_head%d" % a, [P, HEAD_EXPERTS, 2 * H], U8) for a in range(PASSES)]
-        w1_rest = [held("w1_rest%d" % e, [P, PASSES, 2 * H], U8) for e in range(HEAD_EXPERTS, E)]
-        gates = [held("gate%d" % r, [P, T], F32) for r in range(2)]
-        w2_planes = held("w2_planes", [P, E, N], U8)
+        w1_planes = {}
+        w1_head = [held("w1_head%d" % a, [P, PAIR, 2 * H], U8) for a in range(PASSES)]
+        w1_rest = {}
+        gates = held("gates", [P, 2, T], F32)
         w2 = held("w2", [P, E, 2 * N], U8)
         ident = held("ident", [P, P], F32)
         y = held("y", [P, S], F32)
 
-        def load_weight_planes(planes, scales):
+        def load_weight_planes(queue, name, scales):
             rows = scales.rearrange("e s (q r) n -> r q (e s) n", r=4)
+            planes = held(name, [P, rows.shape[2], rows.shape[3]], U8)
             for r in range(4):
-                nc.sync.dma_start(out=planes[r:P:32].bitcast(I32), in_=rows[r].bitcast(I32))
+                queue.dma_start(out=planes[r:P:32].bitcast(I32), in_=rows[r].bitcast(I32))
+            return planes
 
-        def load_x(a):
-            nc.sync.dma_start(out=word_windows[a][:], in_=x_words[a].rearrange("p t r -> p (t r)").bitcast(I32))
+        def load_w1_planes(queue, name, e0, e1):
+            planes = load_weight_planes(queue, name, w1_scales[e0:e1])
+            for e in range(e0, e1):
+                w1_planes[e] = planes[:, (e - e0) * PASSES : (e - e0 + 1) * PASSES, :]
+
+        def load_x(cut):
+            words = x_words[cut[0] : cut[1]].rearrange("a p t r -> p a (t r)")
+            nc.sync.dma_start(out=word_windows[cut[0]][:], in_=words.bitcast(I32))
 
         def load_w1_head(a):
-            words = w1_words[0:HEAD_EXPERTS, a].rearrange("e p b -> p e b")
+            words = w1_words[0:PAIR, a].rearrange("e p b -> p e b")
             nc.sync.dma_start(out=w1_head[a][:].bitcast(I32), in_=words.bitcast(I32))
 
-        def move_first_planes(queue, b):
+        def load_w1_rest(e):
+            for a0, a1 in W1_CUTS:
+                piece = held("w1_rest%d_%d" % (e, a0), [P, a1 - a0, 2 * H], U8)
+                words = w1_words[e, a0:a1].rearrange("s p b -> p s b")
+                nc.sync.dma_start(out=piece[:].bitcast(I32), in_=words.bitcast(I32))
+                w1_rest[e, a0] = piece
+
+        def move_planes(queue, planes, s0, s1):
             for q in QUADS:
                 queue.dma_start(
-                    out=first_planes[b][32 * q : 32 * q + 4].bitcast(I32),
-                    in_=slot_scales[16 * q : 16 * q + 16, b * HEAD : (b + 1) * HEAD].bitcast(I32),
+                    out=planes[32 * q : 32 * q + 4].bitcast(I32),
+                    in_=slot_scales[16 * q : 16 * q + 16, s0:s1].bitcast(I32),
                 )
 
-        def move_last_plane():
+        def move_last_plane(queue):
             for q in QUADS:
-                nc.sync.dma_start(
+                queue.dma_start(
                     out=last_plane[32 * q : 32 * q + 4, :].bitcast(I32),
                     in_=slot_scales[LAST_ROWS + 4 * q : LAST_ROWS + 4 * q + 4, :].bitcast(I32),
                 )
 
         def token_plane(a, j):
+            s0 = j * P
             if a == PASSES - 1:
-                return last_plane[:, j * P : (j + 1) * P]
-            b, s0 = divmod(j * P, HEAD)
-            return first_planes[b][:, a, s0 : s0 + P]
+                return last_plane[:, s0 : s0 + P]
+            if s0 < HEAD:
+                return head_planes[:, a, s0 : s0 + P]
+            return rest_planes[:, a, s0 - HEAD : s0 - HEAD + P]
 
         def w1_operand(e, a):
-            b, within = divmod(e, HEAD_EXPERTS)
-            words = w1_head[a][:, e, :] if b == 0 else w1_rest[within][:, a, :]
-            return words.bitcast(FP4X4), w1_planes[b][:, within * PASSES + a, :]
+            if e < PAIR:
+                words = w1_head[a][:, e, :]
+            else:
+                a0 = cut_of(W1_CUTS, a)
+                words = w1_rest[e, a0][:, a - a0, :]
+            return words.bitcast(FP4X4), w1_planes[e][:, a, :]
+
+        def gather_scales(s0, s1):
+            entries = offs_t[:, s0 // 16 : s1 // 16]
+            nc.vector.tensor_copy(slot_scales[:, s0:s1], scale_window[:].indirect(entries))
+
+        def ring_tile(n):
+            return word_ring.tile([P, n * P], U32, name="slot_words", align_bytes=ALIGN)
+
+        def gather_words(slot_words, tiles, a):
+            a0 = cut_of(X_CUTS, a)
+            entries = offs_t[:, tiles[0] * P // 16 : (tiles[-1] + 1) * P // 16]
+            nc.vector.tensor_copy(slot_words[:], word_windows[a0][:, a - a0, :].bitcast(U32).indirect(entries))
+            return slot_words
 
         nc.vector.memset(scale_window[64:LAST_ROWS, :].bitcast(I32), 0)
         make_identity(nc, ident[:])
@@ -111,118 +148,147 @@ def tile_moe_pkd_mlp_gelu_kernel(
             out=scale_window[0:64, :].bitcast(I32), in_=x_scales[0:4].rearrange("a f t -> f a t").bitcast(I32)
         )
         nc.scalar.dma_start(out=scale_window[LAST_ROWS:P, :].bitcast(I32), in_=x_scales[PASSES - 1].bitcast(I32))
-        for c in range(0, S, GATHER):
-            entries = offs_t[:, c // 16 : (c + GATHER) // 16]
-            nc.vector.tensor_copy(slot_scales[:, c : c + GATHER], scale_window[:].indirect(entries))
 
-        move_first_planes(nc.scalar, 0)
-        load_x(0)
-        load_weight_planes(w1_planes[0], w1_scales[0:HEAD_EXPERTS])
+        expert = [[e * TILES + i for i in range(TILES)] for e in range(E)]
+        head = expert[0] + expert[1]
+        early = {}
+        gather_scales(0, HEAD)
+        move_planes(nc.scalar, head_planes, 0, HEAD)
+        load_x(X_CUTS[0])
+        load_w1_planes(nc.sync, "w1_planes0", 0, 2)
+        load_w1_planes(nc.gpsimd, "w1_planes1", 2, 4)
         load_w1_head(0)
-        load_x(1)
-        for a in range(1, PASSES):
-            if a + 1 < PASSES:
-                load_x(a + 1)
-            else:
-                move_last_plane()
-            load_w1_head(a)
-        move_first_planes(nc.sync, 1)
-        load_weight_planes(w1_planes[1], w1_scales[HEAD_EXPERTS:E])
-        for e in range(HEAD_EXPERTS, E):
-            words = w1_words[e].rearrange("s p b -> p s b")
-            nc.sync.dma_start(out=w1_rest[e - HEAD_EXPERTS][:].bitcast(I32), in_=words.bitcast(I32))
+        early[0, 0] = gather_words(ring_tile(4), head, 0)
+        gather_scales(HEAD, 2 * HEAD)
+        load_x(X_CUTS[1])
+        load_w1_head(1)
+        early[0, 1] = gather_words(ring_tile(4), head, 1)
+        gather_scales(2 * HEAD, S)
+        load_x(X_CUTS[2])
+        load_w1_head(2)
+        load_w1_head(3)
+        move_last_plane(nc.sync)
+        load_w1_head(4)
+        load_w1_rest(2)
+        move_planes(nc.sync, rest_planes, HEAD, S)
+        load_w1_rest(3)
+        load_w1_planes(nc.gpsimd, "scale_window", 4, 6)
+        load_w1_rest(4)
+        load_w1_rest(5)
         nc.sync.dma_start(out=w2[:].bitcast(I32), in_=w2_words[:, 0].rearrange("e p b -> p e b").bitcast(I32))
-        load_weight_planes(w2_planes, w2_scales)
         nc.sync.dma_start(pos1_t[:], pos1)
         nc.sync.dma_start(pos2_t[:], pos2)
-        for r in range(2):
-            nc.sync.dma_start(out=gates[r][:], in_=gate[r])
+        nc.sync.dma_start(out=gates[:], in_=gate.rearrange("r p t -> p r t"))
 
-        def gather_words(j0, n, a):
-            slot_words = word_ring.tile([P, n * P], U32, name="slot_words", align_bytes=ALIGN)
-            for c0 in range(0, n * P, GATHER):
-                c1 = min(c0 + GATHER, n * P)
-                entries = offs_t[:, (j0 * P + c0) // 16 : (j0 * P + c1) // 16]
-                nc.vector.tensor_copy(slot_words[:, c0:c1], word_windows[a][:].bitcast(U32).indirect(entries))
-            return slot_words
+        h = {}
+        gathered = {}
 
-        def first_layer_pass(accs, j0, a, slot_words):
-            for i, acc in enumerate(accs):
-                j = j0 + i
-                w1_codes, w1_plane = w1_operand(j * P // C, a)
-                nc.tensor.matmul_mx(
-                    out=acc[:],
-                    lhsT=slot_words[:, i * P : (i + 1) * P].bitcast(FP8X4),
-                    lhsT_scale=token_plane(a, j),
-                    rhs=w1_codes,
-                    rhs_scale=w1_plane,
-                    start=(a == 0),
-                    stop=(a == PASSES - 1),
-                )
-
-        def activate(j, acc):
-            h = held("h%d" % j, [P, H], BF16)
-            step = 1 if j == LAST_TILE else 2
+        def activate(j, acc, step):
+            h[j] = held("h%d" % j, [P, H], BF16)
             for u in range(0, 2, step):
                 nc.scalar.activation(
-                    out=h[:].rearrange("s (u p d) -> s u p d", u=2, d=2)[:, u : u + step],
+                    out=h[j][:].rearrange("s (u p d) -> s u p d", u=2, d=2)[:, u : u + step],
                     in_=acc[:].rearrange("s (p u d) -> s u p d", u=2, d=2)[:, u : u + step],
                     func=GELU,
                 )
-            return h
 
-        turned_groups = []
-
-        def turn_groups(groups):
-            for j, group in groups:
-                n = len(group)
-                h_turned = held("h_turned%d" % j, [P, n * H], BF16)
-                bank = turn_pool.tile([P, n, 2, P], F32, name="bank")
-                for i, h in enumerate(group):
-                    pairs = h[:].bitcast(F32)
-                    for u in range(2):
-                        nc.tensor.transpose(bank[:, i, u, :], pairs[:, u * P : (u + 1) * P], ident[:])
-                nc.scalar.copy(
-                    out=h_turned[:].bitcast(F32).rearrange("p (i s u) -> p i s u", i=n, u=2),
-                    in_=bank[:].rearrange("p i u s -> p i s u"),
-                )
-                turned_groups.append((j, n, h_turned))
-
-        waiting = []
-        for j0, n in CHUNKS:
-            accs = [acc_pool.tile([P, H], F32, name="acc") for i in range(n)]
+        def first_layer(tiles, first_bank, step=2, first_words=None):
+            accs = [bank_tile(first_bank + i, [P, H]) for i in range(len(tiles))]
             for a in range(PASSES):
-                first_layer_pass(accs, j0, a, gather_words(j0, n, a))
-            h_tiles = [activate(j0 + i, acc) for i, acc in enumerate(accs)]
-            turn_groups(waiting)
-            waiting = [(j0 + i, h_tiles[i : i + 2]) for i in range(0, n, 2)]
-        turn_groups(waiting)
+                if (tiles[0], a) in early:
+                    slot_words = early[tiles[0], a]
+                elif a == 0 and first_words is not None:
+                    slot_words = gather_words(held(first_words, [P, len(tiles) * P], U32), tiles, a)
+                else:
+                    slot_words = gather_words(ring_tile(len(tiles)), tiles, a)
+                gathered[tiles[0], a] = slot_words
+                for i, j in enumerate(tiles):
+                    w1_codes, w1_plane = w1_operand(j // TILES, a)
+                    nc.tensor.matmul_mx(
+                        out=accs[i][:],
+                        lhsT=slot_words[:, i * P : (i + 1) * P].bitcast(FP8X4),
+                        lhsT_scale=token_plane(a, j),
+                        rhs=w1_codes,
+                        rhs_scale=w1_plane,
+                        start=(a == 0),
+                        stop=(a == PASSES - 1),
+                    )
+            for j, acc in zip(tiles, accs):
+                activate(j, acc, step)
 
-        h_words = held("word_window%d" % (PASSES - 1), [P, S], U32)
-        h_plane = held("h_plane", [P, S], U8)
-        for j, n, h_turned in turned_groups:
-            s0, s1 = j * P, (j + n) * P
-            nc.vector.quantize_mx(out=h_words[:, s0:s1].bitcast(FP8X4), scales=h_plane[:, s0:s1], in_=h_turned[:])
-            y_bank = acc_pool.tile([P, n * P], F32, name="acc")
-            nc.tensor.matmul_mx(
-                out=y_bank[:],
-                lhsT=w2[:, s0 // C, :].bitcast(FP4X4),
-                lhsT_scale=w2_planes[:, s0 // C, :],
-                rhs=h_words[:, s0:s1].bitcast(FP8X4),
-                rhs_scale=h_plane[:, s0:s1],
-                start=True,
-                stop=True,
+        turned = {}
+
+        def turn(tiles, b, copy):
+            n = len(tiles)
+            h_turned = held("h_turned%d" % tiles[0], [P, n * H], BF16)
+            bank = bank_tile(b, [P, n, 2, P])
+            for i, j in enumerate(tiles):
+                pairs = h[j][:].bitcast(F32)
+                for u in range(2):
+                    nc.tensor.transpose(bank[:, i, u, :], pairs[:, u * P : (u + 1) * P], ident[:])
+            copy(
+                out=h_turned[:].bitcast(F32).rearrange("p (i s u) -> p i s u", i=n, u=2),
+                in_=bank[:].rearrange("p i u s -> p i s u"),
             )
-            if s0 // C < E - 2:
-                nc.scalar.copy(out=y[:, s0:s1], in_=y_bank[:])
-            else:
-                nc.vector.tensor_copy(out=y[:, s0:s1], in_=y_bank[:])
+            turned[tiles[0]] = h_turned
+
+        codes = {}
+
+        def quantize(tiles, h_plane):
+            s0, s1 = tiles[0] * P, (tiles[-1] + 1) * P
+            h_words = held("h_words%d" % tiles[0], [P, s1 - s0], U32)
+            nc.vector.quantize_mx(out=h_words[:].bitcast(FP8X4), scales=h_plane[:, s0:s1], in_=turned[tiles[0]][:])
+            codes[tiles[0]] = (h_words, h_plane[:, s0:s1])
+
+        def second_layer(groups, b, copy):
+            s_first, s_last = groups[0][0] * P, (groups[-1][-1] + 1) * P
+            y_bank = bank_tile(b, [P, s_last - s_first])
+            for tiles in groups:
+                s0, s1 = tiles[0] * P, (tiles[-1] + 1) * P
+                nc.tensor.matmul_mx(
+                    out=y_bank[:, s0 - s_first : s1 - s_first],
+                    lhsT=w2[:, s0 // C, :].bitcast(FP4X4),
+                    lhsT_scale=w2_planes[:, s0 // C, :],
+                    rhs=codes[tiles[0]][0][:].bitcast(FP8X4),
+                    rhs_scale=codes[tiles[0]][1],
+                    start=True,
+                    stop=True,
+                )
+            copy(out=y[:, s_first:s_last], in_=y_bank[:])
+
+        on_scalar, on_vector = nc.scalar.copy, nc.vector.tensor_copy
+        first_layer(head, 0)
+        w2_planes = load_weight_planes(nc.gpsimd, "head_planes", w2_scales)
+        first_layer(expert[2], 4)
+        first_layer(expert[3], 6)
+        turn(expert[0], 4, on_scalar)
+        turn(expert[1], 5, on_scalar)
+        first_layer(expert[4], 0)
+        turn(expert[2], 6, on_scalar)
+        turn(expert[3], 7, on_scalar)
+        first_layer([10], 2, first_words="w1_rest3_0")
+        h_plane = held("w1_rest3_0", [P, S], U8)
+        first_layer([11], 3, step=1)
+        for e in range(4):
+            quantize(expert[e], h_plane)
+        turn(expert[4], 2, on_vector)
+        turn([10], 0, on_vector)
+        second_layer([expert[0], expert[1]], 1, on_scalar)
+        second_layer([expert[2], expert[3]], 4, on_scalar)
+        quantize(expert[4], h_plane)
+        turn([11], 5, on_vector)
+        quantize([10], h_plane)
+        second_layer([expert[4]], 6, on_scalar)
+        quantize([11], h_plane)
+        second_layer([[10]], 7, on_scalar)
+        second_layer([[11]], 3, on_vector)
+
 
         first = held("first", [P, T], F32)
-        nc.vector.tensor_tensor(first[:], y[:].indirect(pos1_t[:]), gates[0][:], MULT)
+        nc.vector.tensor_tensor(first[:], y[:].indirect(pos1_t[:]), gates[:, 0, :], MULT)
         for t0, t1 in ((0, T // 2), (T // 2, T)):
             second = held("second%d" % t0, [P, t1 - t0], F32)
             total = held("total%d" % t0, [P, t1 - t0], F32)
-            nc.vector.tensor_tensor(second[:], y[:].indirect(pos2_t[:, t0 // 16 : t1 // 16]), gates[1][:, t0:t1], MULT)
+            nc.vector.tensor_tensor(second[:], y[:].indirect(pos2_t[:, t0 // 16 : t1 // 16]), gates[:, 1, t0:t1], MULT)
             nc.vector.tensor_tensor(total[:], first[:, t0:t1], second[:], ADD)
             nc.sync.dma_start(out=out[:, t0:t1], in_=total[:])

@@ -27,7 +27,7 @@ HEAD = PAIR * C
 TILES = C // P
 WORD_BUFS = 12
 X_CUTS = ((0, 1), (1, 3), (3, PASSES))
-W1_CUTS = ((0, PASSES),)
+W1_CUTS = {2: ((0, 2), (2, PASSES)), 3: ((0, PASSES),), 4: ((0, PASSES),), 5: ((0, PASSES),)}
 QUADS = (0, 2, 1, 3)
 LAST_ROWS = P - 16
 
@@ -90,8 +90,8 @@ def tile_moe_pkd_mlp_gelu_kernel(
             words = w1_words[0:PAIR, a].rearrange("e p b -> p e b")
             nc.sync.dma_start(out=w1_head[a][:].bitcast(I32), in_=words.bitcast(I32))
 
-        def load_w1_rest(e):
-            for a0, a1 in W1_CUTS:
+        def load_w1_rest(e, cuts=None):
+            for a0, a1 in cuts or W1_CUTS[e]:
                 piece = held("w1_rest%d_%d" % (e, a0), [P, a1 - a0, 2 * H], U8)
                 words = w1_words[e, a0:a1].rearrange("s p b -> p s b")
                 nc.sync.dma_start(out=piece[:].bitcast(I32), in_=words.bitcast(I32))
@@ -123,7 +123,7 @@ def tile_moe_pkd_mlp_gelu_kernel(
             if e < PAIR:
                 words = w1_head[a][:, e, :]
             else:
-                a0 = cut_of(W1_CUTS, a)
+                a0 = cut_of(W1_CUTS[e], a)
                 words = w1_rest[e, a0][:, a - a0, :]
             return words.bitcast(FP4X4), w1_planes[e][:, a, :]
 
@@ -155,8 +155,7 @@ def tile_moe_pkd_mlp_gelu_kernel(
         gather_scales(0, HEAD)
         move_planes(nc.scalar, head_planes, 0, HEAD)
         load_x(X_CUTS[0])
-        load_w1_planes(nc.sync, "w1_planes0", 0, 2)
-        load_w1_planes(nc.gpsimd, "w1_planes1", 2, 4)
+        load_w1_planes(nc.sync, "w1_planes0", 0, 4)
         load_w1_head(0)
         early[0, 0] = gather_words(ring_tile(4), head, 0)
         gather_scales(HEAD, 2 * HEAD)
@@ -169,13 +168,15 @@ def tile_moe_pkd_mlp_gelu_kernel(
         load_w1_head(3)
         move_last_plane(nc.sync)
         load_w1_head(4)
-        load_w1_rest(2)
+        load_w1_rest(2, W1_CUTS[2][:1])
         move_planes(nc.sync, rest_planes, HEAD, S)
+        load_w1_rest(2, W1_CUTS[2][1:])
         load_w1_rest(3)
-        load_w1_planes(nc.gpsimd, "scale_window", 4, 6)
+        load_w1_planes(nc.sync, "w1_planes1", 4, 6)
         load_w1_rest(4)
         load_w1_rest(5)
         nc.sync.dma_start(out=w2[:].bitcast(I32), in_=w2_words[:, 0].rearrange("e p b -> p e b").bitcast(I32))
+        w2_planes = load_weight_planes(nc.sync, "w2_planes", w2_scales)
         nc.sync.dma_start(pos1_t[:], pos1)
         nc.sync.dma_start(pos2_t[:], pos2)
         nc.sync.dma_start(out=gates[:], in_=gate.rearrange("r p t -> p r t"))
@@ -258,7 +259,6 @@ def tile_moe_pkd_mlp_gelu_kernel(
 
         on_scalar, on_vector = nc.scalar.copy, nc.vector.tensor_copy
         first_layer(head, 0)
-        w2_planes = load_weight_planes(nc.gpsimd, "head_planes", w2_scales)
         first_layer(expert[2], 4)
         first_layer(expert[3], 6)
         turn(expert[0], 4, on_scalar)

@@ -24,10 +24,11 @@ ADD = mybir.AluOpType.add
 ALIGN = 256
 PAIR = 2
 HEAD = PAIR * C
+HALF = S // 2
 TILES = C // P
-WORD_BUFS = 12
-X_CUTS = ((0, 1), (1, 3), (3, PASSES))
-W1_CUTS = {2: ((0, 2), (2, PASSES)), 3: ((0, PASSES),), 4: ((0, PASSES),), 5: ((0, PASSES),)}
+WORD_BUFS = 8
+X_CUTS = ((0, 1), (1, 2), (2, 3), (3, 4), (4, PASSES))
+W1_CUTS = {2: ((0, 2), (2, PASSES)), 3: ((0, 2), (2, PASSES)), 4: ((0, PASSES),), 5: ((0, PASSES),)}
 QUADS = (0, 2, 1, 3)
 LAST_ROWS = P - 16
 
@@ -59,26 +60,26 @@ def tile_moe_pkd_mlp_gelu_kernel(
         scale_window = held("scale_window", [P, T], U8)
         word_windows = {a0: held("word_window%d" % a0, [P, a1 - a0, T], I32) for a0, a1 in X_CUTS}
         slot_scales = held("slot_scales", [P, S], U8)
-        head_planes = held("head_planes", [P, 4, HEAD], U8)
-        rest_planes = held("rest_planes", [P, 4, S - HEAD], U8)
+        head_planes = held("head_planes", [P, 4, HALF], U8)
+        rest_planes = held("rest_planes", [P, 4, S - HALF], U8)
         last_plane = held("last_plane", [P, S], U8)
         w1_planes = {}
-        w1_head = [held("w1_head%d" % a, [P, PAIR, 2 * H], U8) for a in range(PASSES)]
+        w1_head = {}
         w1_rest = {}
         gates = held("gates", [P, 2, T], F32)
         w2 = held("w2", [P, E, 2 * N], U8)
         ident = held("ident", [P, P], F32)
         y = held("y", [P, S], F32)
 
-        def load_weight_planes(queue, name, scales):
+        def load_weight_planes(queues, name, scales):
             rows = scales.rearrange("e s (q r) n -> r q (e s) n", r=4)
             planes = held(name, [P, rows.shape[2], rows.shape[3]], U8)
             for r in range(4):
-                queue.dma_start(out=planes[r:P:32].bitcast(I32), in_=rows[r].bitcast(I32))
+                queues[r].dma_start(out=planes[r:P:32].bitcast(I32), in_=rows[r].bitcast(I32))
             return planes
 
-        def load_w1_planes(queue, name, e0, e1):
-            planes = load_weight_planes(queue, name, w1_scales[e0:e1])
+        def load_w1_planes(queues, name, e0, e1):
+            planes = load_weight_planes(queues, name, w1_scales[e0:e1])
             for e in range(e0, e1):
                 w1_planes[e] = planes[:, (e - e0) * PASSES : (e - e0 + 1) * PASSES, :]
 
@@ -87,6 +88,10 @@ def tile_moe_pkd_mlp_gelu_kernel(
             nc.sync.dma_start(out=word_windows[cut[0]][:], in_=words.bitcast(I32))
 
         def load_w1_head(a):
+            if a < 2:
+                w1_head[a] = held("w1_head%d" % a, [P, PAIR, 2 * H], U8)
+            else:
+                w1_head[a] = word_ring.tile([P, PAIR, 2 * H], U8, name="slot_words", align_bytes=ALIGN)
             words = w1_words[0:PAIR, a].rearrange("e p b -> p e b")
             nc.sync.dma_start(out=w1_head[a][:].bitcast(I32), in_=words.bitcast(I32))
 
@@ -115,9 +120,9 @@ def tile_moe_pkd_mlp_gelu_kernel(
             s0 = j * P
             if a == PASSES - 1:
                 return last_plane[:, s0 : s0 + P]
-            if s0 < HEAD:
+            if s0 < HALF:
                 return head_planes[:, a, s0 : s0 + P]
-            return rest_planes[:, a, s0 - HEAD : s0 - HEAD + P]
+            return rest_planes[:, a, s0 - HALF : s0 - HALF + P]
 
         def w1_operand(e, a):
             if e < PAIR:
@@ -136,12 +141,15 @@ def tile_moe_pkd_mlp_gelu_kernel(
 
         def gather_words(slot_words, tiles, a):
             a0 = cut_of(X_CUTS, a)
-            entries = offs_t[:, tiles[0] * P // 16 : (tiles[-1] + 1) * P // 16]
-            nc.vector.tensor_copy(slot_words[:], word_windows[a0][:, a - a0, :].bitcast(U32).indirect(entries))
+            window = word_windows[a0][:, a - a0, :].bitcast(U32)
+            step = len(tiles) if a < 2 else TILES
+            for i in range(0, len(tiles), step):
+                part = tiles[i : i + step]
+                entries = offs_t[:, part[0] * P // 16 : (part[-1] + 1) * P // 16]
+                nc.vector.tensor_copy(slot_words[:, i * P : (i + len(part)) * P], window.indirect(entries))
             return slot_words
 
         nc.vector.memset(scale_window[64:LAST_ROWS, :].bitcast(I32), 0)
-        make_identity(nc, ident[:])
 
         nc.sync.dma_start(offs_t[:], offs)
         nc.scalar.dma_start(
@@ -152,31 +160,35 @@ def tile_moe_pkd_mlp_gelu_kernel(
         expert = [[e * TILES + i for i in range(TILES)] for e in range(E)]
         head = expert[0] + expert[1]
         early = {}
-        gather_scales(0, HEAD)
-        move_planes(nc.scalar, head_planes, 0, HEAD)
+        gather_scales(0, 384)
+        gather_scales(384, HALF)
+        move_planes(nc.scalar, head_planes, 0, HALF)
         load_x(X_CUTS[0])
-        load_w1_planes(nc.sync, "w1_planes0", 0, 4)
+        load_w1_planes([nc.gpsimd, nc.gpsimd, nc.sync, nc.sync], "w1_planes0", 0, 3)
+        nc.vector.memset(ident[:], 0.0)
+        make_identity(nc, ident[:], nomemset=True)
         load_w1_head(0)
-        early[0, 0] = gather_words(ring_tile(4), head, 0)
-        gather_scales(HEAD, 2 * HEAD)
+        early[0, 0] = gather_words(held("head_words0", [P, HEAD], U32), head, 0)
+        gather_scales(HALF, HALF + 384)
         load_x(X_CUTS[1])
-        load_w1_head(1)
-        early[0, 1] = gather_words(ring_tile(4), head, 1)
-        gather_scales(2 * HEAD, S)
         load_x(X_CUTS[2])
+        load_w1_head(1)
+        early[0, 1] = gather_words(held("head_words1", [P, HEAD], U32), head, 1)
+        gather_scales(HALF + 384, S)
+        load_x(X_CUTS[3])
         load_w1_head(2)
+        load_x(X_CUTS[4])
         load_w1_head(3)
         move_last_plane(nc.sync)
         load_w1_head(4)
-        load_w1_rest(2, W1_CUTS[2][:1])
-        move_planes(nc.sync, rest_planes, HEAD, S)
-        load_w1_rest(2, W1_CUTS[2][1:])
+        load_w1_rest(2)
+        move_planes(nc.sync, rest_planes, HALF, S)
+        load_w1_planes([nc.sync] * 4, "w1_planes1", 3, 6)
         load_w1_rest(3)
-        load_w1_planes(nc.sync, "w1_planes1", 4, 6)
         load_w1_rest(4)
         load_w1_rest(5)
         nc.sync.dma_start(out=w2[:].bitcast(I32), in_=w2_words[:, 0].rearrange("e p b -> p e b").bitcast(I32))
-        w2_planes = load_weight_planes(nc.sync, "w2_planes", w2_scales)
+        w2_planes = load_weight_planes([nc.sync] * 4, "w2_planes", w2_scales)
         nc.sync.dma_start(pos1_t[:], pos1)
         nc.sync.dma_start(pos2_t[:], pos2)
         nc.sync.dma_start(out=gates[:], in_=gate.rearrange("r p t -> p r t"))
@@ -193,29 +205,30 @@ def tile_moe_pkd_mlp_gelu_kernel(
                     func=GELU,
                 )
 
-        def first_layer(tiles, first_bank, step=2, first_words=None):
+        def first_layer(tiles, first_bank, order=None, first_words=None):
             accs = [bank_tile(first_bank + i, [P, H]) for i in range(len(tiles))]
-            for a in range(PASSES):
-                if (tiles[0], a) in early:
-                    slot_words = early[tiles[0], a]
-                elif a == 0 and first_words is not None:
-                    slot_words = gather_words(held(first_words, [P, len(tiles) * P], U32), tiles, a)
-                else:
-                    slot_words = gather_words(ring_tile(len(tiles)), tiles, a)
-                gathered[tiles[0], a] = slot_words
-                for i, j in enumerate(tiles):
-                    w1_codes, w1_plane = w1_operand(j // TILES, a)
-                    nc.tensor.matmul_mx(
-                        out=accs[i][:],
-                        lhsT=slot_words[:, i * P : (i + 1) * P].bitcast(FP8X4),
-                        lhsT_scale=token_plane(a, j),
-                        rhs=w1_codes,
-                        rhs_scale=w1_plane,
-                        start=(a == 0),
-                        stop=(a == PASSES - 1),
-                    )
-            for j, acc in zip(tiles, accs):
-                activate(j, acc, step)
+            words = {}
+            for i, a in order or [(i, a) for a in range(PASSES) for i in range(len(tiles))]:
+                if a not in words:
+                    if (tiles[0], a) in early:
+                        words[a] = early[tiles[0], a]
+                    elif a == 0 and first_words is not None:
+                        words[a] = gather_words(held(first_words, [P, len(tiles) * P], U32), tiles, a)
+                    else:
+                        words[a] = gather_words(ring_tile(len(tiles)), tiles, a)
+                j = tiles[i]
+                w1_codes, w1_plane = w1_operand(j // TILES, a)
+                nc.tensor.matmul_mx(
+                    out=accs[i][:],
+                    lhsT=words[a][:, i * P : (i + 1) * P].bitcast(FP8X4),
+                    lhsT_scale=token_plane(a, j),
+                    rhs=w1_codes,
+                    rhs_scale=w1_plane,
+                    start=(a == 0),
+                    stop=(a == PASSES - 1),
+                )
+                if a == PASSES - 1:
+                    activate(j, accs[i], 1 if j == S // P - 1 else 2)
 
         turned = {}
 
@@ -258,37 +271,59 @@ def tile_moe_pkd_mlp_gelu_kernel(
             copy(out=y[:, s_first:s_last], in_=y_bank[:])
 
         on_scalar, on_vector = nc.scalar.copy, nc.vector.tensor_copy
+        warm_bank = bank_tile(7, [P, H])
+        for i in range(3):
+            w1_codes, w1_plane = w1_operand(0, 0)
+            nc.tensor.matmul_mx(
+                out=warm_bank[:],
+                lhsT=early[0, 0][:, 0:P].bitcast(FP8X4),
+                lhsT_scale=slot_scales[:, 0:P],
+                rhs=w1_codes,
+                rhs_scale=slot_scales[:, 0:H],
+                start=True,
+                stop=True,
+            )
         first_layer(head, 0)
         first_layer(expert[2], 4)
+        turn(expert[0], 0, on_scalar)
+        turn(expert[1], 1, on_scalar)
         first_layer(expert[3], 6)
-        turn(expert[0], 4, on_scalar)
-        turn(expert[1], 5, on_scalar)
-        first_layer(expert[4], 0)
-        turn(expert[2], 6, on_scalar)
-        turn(expert[3], 7, on_scalar)
-        first_layer([10], 2, first_words="w1_rest3_0")
+        first_layer(expert[4], 2)
+        turn(expert[2], 4, on_scalar)
+        turn(expert[3], 5, on_scalar)
+        last_order = [(i, 0) for i in range(TILES)] + [(i, a) for i in range(TILES) for a in range(1, PASSES)]
+        first_layer(expert[5], 6, order=last_order, first_words="w1_rest3_0")
         h_plane = held("w1_rest3_0", [P, S], U8)
-        first_layer([11], 3, step=1)
         for e in range(4):
             quantize(expert[e], h_plane)
-        turn(expert[4], 2, on_vector)
+        turn(expert[4], 6, on_vector)
         turn([10], 0, on_vector)
         second_layer([expert[0], expert[1]], 1, on_scalar)
         second_layer([expert[2], expert[3]], 4, on_scalar)
         quantize(expert[4], h_plane)
         turn([11], 5, on_vector)
         quantize([10], h_plane)
-        second_layer([expert[4]], 6, on_scalar)
+        second_layer([expert[4]], 2, on_scalar)
         quantize([11], h_plane)
-        second_layer([[10]], 7, on_scalar)
-        second_layer([[11]], 3, on_vector)
+        second_layer([[10]], 3, on_scalar)
+        second_layer([[11]], 7, on_vector)
 
 
-        first = held("first", [P, T], F32)
-        nc.vector.tensor_tensor(first[:], y[:].indirect(pos1_t[:]), gates[:, 0, :], MULT)
-        for t0, t1 in ((0, T // 2), (T // 2, T)):
-            second = held("second%d" % t0, [P, t1 - t0], F32)
+        def fetch(r, pos_t, t0, t1):
+            picked = held("picked%d_%d" % (r, t0), [P, t1 - t0], F32)
+            nc.vector.tensor_tensor(picked[:], y[:].indirect(pos_t[:, t0 // 16 : t1 // 16]), gates[:, r, t0:t1], MULT)
+            return picked
+
+        def add_and_store(queue, t0, t1, pair):
             total = held("total%d" % t0, [P, t1 - t0], F32)
-            nc.vector.tensor_tensor(second[:], y[:].indirect(pos2_t[:, t0 // 16 : t1 // 16]), gates[:, 1, t0:t1], MULT)
-            nc.vector.tensor_tensor(total[:], first[:, t0:t1], second[:], ADD)
-            nc.sync.dma_start(out=out[:, t0:t1], in_=total[:])
+            nc.vector.tensor_tensor(total[:], pair[0][:], pair[1][:], ADD)
+            queue.dma_start(out=out[:, t0:t1], in_=total[:])
+
+        a0, a1, a2, a3 = 0, 384, 640, T
+        pair_a = [fetch(0, pos1_t, a0, a1), fetch(1, pos2_t, a0, a1)]
+        first_b = fetch(0, pos1_t, a1, a2)
+        add_and_store(nc.sync, a0, a1, pair_a)
+        pair_b = [first_b, fetch(1, pos2_t, a1, a2)]
+        pair_c = [fetch(0, pos1_t, a2, a3), fetch(1, pos2_t, a2, a3)]
+        add_and_store(nc.sync, a1, a2, pair_b)
+        add_and_store(nc.scalar, a2, a3, pair_c)

@@ -22,19 +22,20 @@ MULT = mybir.AluOpType.mult
 ADD = mybir.AluOpType.add
 
 ALIGN = 256
-PAIR = 2
-HEAD = PAIR * C
-HALF = S // 2
 TILES = C // P
+LAST_TILE = S // P - 1
+HEAD_EXPERTS = 2
+HEAD = HEAD_EXPERTS * C
+HALF = S // 2
+BYTE_GATHER = HALF // 2
+WIDE_PASSES = 2
 WORD_BUFS = 8
-X_CUTS = ((0, 1), (1, 2), (2, 3), (3, 4), (4, PASSES))
-W1_CUTS = {2: ((0, 2), (2, PASSES)), 3: ((0, 2), (2, PASSES)), 4: ((0, PASSES),), 5: ((0, PASSES),)}
+SPLIT, WHOLE = ((0, 2), (2, PASSES)), ((0, PASSES),)
+W1_CUTS = {2: SPLIT, 3: SPLIT, 4: WHOLE, 5: WHOLE}
+LATE_BUFFER = "w1_expert3_0"
 QUADS = (0, 2, 1, 3)
 LAST_ROWS = P - 16
-
-
-def cut_of(cuts, a):
-    return max(a0 for a0, a1 in cuts if a0 <= a)
+TOKEN_CUTS = (0, T // 2, T - P, T)
 
 
 def tile_moe_pkd_mlp_gelu_kernel(
@@ -50,6 +51,9 @@ def tile_moe_pkd_mlp_gelu_kernel(
         def held(name, shape, dtype):
             return keep.tile(shape, dtype, name=name, align_bytes=ALIGN)
 
+        def ring_tile(shape, dtype):
+            return word_ring.tile(shape, dtype, name="ring", align_bytes=ALIGN)
+
         def bank_tile(b, shape):
             return banks.tile(shape, F32, name="bank%d" % b)
 
@@ -58,96 +62,75 @@ def tile_moe_pkd_mlp_gelu_kernel(
         pos2_t = lists.tile([P, T // 16], U16, name="pos2_t")
 
         scale_window = held("scale_window", [P, T], U8)
-        word_windows = {a0: held("word_window%d" % a0, [P, a1 - a0, T], I32) for a0, a1 in X_CUTS}
+        word_windows = [held("word_window%d" % a, [P, T], I32) for a in range(PASSES)]
         slot_scales = held("slot_scales", [P, S], U8)
-        head_planes = held("head_planes", [P, 4, HALF], U8)
-        rest_planes = held("rest_planes", [P, 4, S - HALF], U8)
+        first_planes = [held("first_planes%d" % b, [P, 4, HALF], U8) for b in range(2)]
         last_plane = held("last_plane", [P, S], U8)
-        w1_planes = {}
-        w1_head = {}
-        w1_rest = {}
         gates = held("gates", [P, 2, T], F32)
         w2 = held("w2", [P, E, 2 * N], U8)
         ident = held("ident", [P, P], F32)
         y = held("y", [P, S], F32)
+        w1_planes = []
+        w1_codes = {}
 
         def load_weight_planes(queues, name, scales):
             rows = scales.rearrange("e s (q r) n -> r q (e s) n", r=4)
             planes = held(name, [P, rows.shape[2], rows.shape[3]], U8)
-            for r in range(4):
-                queues[r].dma_start(out=planes[r:P:32].bitcast(I32), in_=rows[r].bitcast(I32))
+            for r, queue in enumerate(queues):
+                queue.dma_start(out=planes[r:P:32].bitcast(I32), in_=rows[r].bitcast(I32))
             return planes
 
-        def load_w1_planes(queues, name, e0, e1):
-            planes = load_weight_planes(queues, name, w1_scales[e0:e1])
-            for e in range(e0, e1):
-                w1_planes[e] = planes[:, (e - e0) * PASSES : (e - e0 + 1) * PASSES, :]
+        def load_w1_planes(queues, b):
+            scales = w1_scales[b * E // 2 : (b + 1) * E // 2]
+            w1_planes.append(load_weight_planes(queues, "w1_planes%d" % b, scales))
 
-        def load_x(cut):
-            words = x_words[cut[0] : cut[1]].rearrange("a p t r -> p a (t r)")
-            nc.sync.dma_start(out=word_windows[cut[0]][:], in_=words.bitcast(I32))
+        def load_x(a):
+            nc.sync.dma_start(out=word_windows[a][:], in_=x_words[a].rearrange("p t r -> p (t r)").bitcast(I32))
 
         def load_w1_head(a):
-            if a < 2:
-                w1_head[a] = held("w1_head%d" % a, [P, PAIR, 2 * H], U8)
-            else:
-                w1_head[a] = word_ring.tile([P, PAIR, 2 * H], U8, name="slot_words", align_bytes=ALIGN)
-            words = w1_words[0:PAIR, a].rearrange("e p b -> p e b")
-            nc.sync.dma_start(out=w1_head[a][:].bitcast(I32), in_=words.bitcast(I32))
+            shape = [P, HEAD_EXPERTS, 2 * H]
+            piece = held("w1_head%d" % a, shape, U8) if a < WIDE_PASSES else ring_tile(shape, U8)
+            words = w1_words[0:HEAD_EXPERTS, a].rearrange("e p b -> p e b")
+            nc.sync.dma_start(out=piece[:].bitcast(I32), in_=words.bitcast(I32))
+            for e in range(HEAD_EXPERTS):
+                w1_codes[e, a] = piece[:, e, :]
 
-        def load_w1_rest(e, cuts=None):
-            for a0, a1 in cuts or W1_CUTS[e]:
-                piece = held("w1_rest%d_%d" % (e, a0), [P, a1 - a0, 2 * H], U8)
+        def load_w1_expert(e):
+            for a0, a1 in W1_CUTS[e]:
+                piece = held("w1_expert%d_%d" % (e, a0), [P, a1 - a0, 2 * H], U8)
                 words = w1_words[e, a0:a1].rearrange("s p b -> p s b")
                 nc.sync.dma_start(out=piece[:].bitcast(I32), in_=words.bitcast(I32))
-                w1_rest[e, a0] = piece
+                for a in range(a0, a1):
+                    w1_codes[e, a] = piece[:, a - a0, :]
 
-        def move_planes(queue, planes, s0, s1):
+        def move_first_planes(queue, b):
             for q in QUADS:
                 queue.dma_start(
-                    out=planes[32 * q : 32 * q + 4].bitcast(I32),
-                    in_=slot_scales[16 * q : 16 * q + 16, s0:s1].bitcast(I32),
+                    out=first_planes[b][32 * q : 32 * q + 4].bitcast(I32),
+                    in_=slot_scales[16 * q : 16 * q + 16, b * HALF : (b + 1) * HALF].bitcast(I32),
                 )
 
-        def move_last_plane(queue):
+        def move_last_plane():
             for q in QUADS:
-                queue.dma_start(
+                nc.sync.dma_start(
                     out=last_plane[32 * q : 32 * q + 4, :].bitcast(I32),
                     in_=slot_scales[LAST_ROWS + 4 * q : LAST_ROWS + 4 * q + 4, :].bitcast(I32),
                 )
 
-        def token_plane(a, j):
-            s0 = j * P
-            if a == PASSES - 1:
-                return last_plane[:, s0 : s0 + P]
-            if s0 < HALF:
-                return head_planes[:, a, s0 : s0 + P]
-            return rest_planes[:, a, s0 - HALF : s0 - HALF + P]
+        def gather_scales(g):
+            s0, s1 = g * BYTE_GATHER, (g + 1) * BYTE_GATHER
+            nc.vector.tensor_copy(slot_scales[:, s0:s1], scale_window[:].indirect(offs_t[:, s0 // 16 : s1 // 16]))
 
-        def w1_operand(e, a):
-            if e < PAIR:
-                words = w1_head[a][:, e, :]
-            else:
-                a0 = cut_of(W1_CUTS[e], a)
-                words = w1_rest[e, a0][:, a - a0, :]
-            return words.bitcast(FP4X4), w1_planes[e][:, a, :]
-
-        def gather_scales(s0, s1):
+        def gather_words(slot_words, s0, s1, a):
             entries = offs_t[:, s0 // 16 : s1 // 16]
-            nc.vector.tensor_copy(slot_scales[:, s0:s1], scale_window[:].indirect(entries))
+            nc.vector.tensor_copy(slot_words, word_windows[a][:].bitcast(U32).indirect(entries))
 
-        def ring_tile(n):
-            return word_ring.tile([P, n * P], U32, name="slot_words", align_bytes=ALIGN)
+        head_words = []
 
-        def gather_words(slot_words, tiles, a):
-            a0 = cut_of(X_CUTS, a)
-            window = word_windows[a0][:, a - a0, :].bitcast(U32)
-            step = len(tiles) if a < 2 else TILES
-            for i in range(0, len(tiles), step):
-                part = tiles[i : i + step]
-                entries = offs_t[:, part[0] * P // 16 : (part[-1] + 1) * P // 16]
-                nc.vector.tensor_copy(slot_words[:, i * P : (i + len(part)) * P], window.indirect(entries))
-            return slot_words
+        def gather_wide(a):
+            slot_words = held("head_words%d" % a, [P, HEAD], U32)
+            gather_words(slot_words[:], 0, HEAD, a)
+            head_words.append(slot_words)
 
         nc.vector.memset(scale_window[64:LAST_ROWS, :].bitcast(I32), 0)
 
@@ -156,48 +139,73 @@ def tile_moe_pkd_mlp_gelu_kernel(
             out=scale_window[0:64, :].bitcast(I32), in_=x_scales[0:4].rearrange("a f t -> f a t").bitcast(I32)
         )
         nc.scalar.dma_start(out=scale_window[LAST_ROWS:P, :].bitcast(I32), in_=x_scales[PASSES - 1].bitcast(I32))
-
-        expert = [[e * TILES + i for i in range(TILES)] for e in range(E)]
-        head = expert[0] + expert[1]
-        early = {}
-        gather_scales(0, 384)
-        gather_scales(384, HALF)
-        move_planes(nc.scalar, head_planes, 0, HALF)
-        load_x(X_CUTS[0])
-        load_w1_planes([nc.gpsimd, nc.gpsimd, nc.sync, nc.sync], "w1_planes0", 0, 3)
+        gather_scales(0)
+        gather_scales(1)
+        move_first_planes(nc.scalar, 0)
+        load_x(0)
+        load_w1_planes([nc.gpsimd, nc.gpsimd, nc.sync, nc.sync], 0)
         nc.vector.memset(ident[:], 0.0)
         make_identity(nc, ident[:], nomemset=True)
         load_w1_head(0)
-        early[0, 0] = gather_words(held("head_words0", [P, HEAD], U32), head, 0)
-        gather_scales(HALF, HALF + 384)
-        load_x(X_CUTS[1])
-        load_x(X_CUTS[2])
+        gather_wide(0)
+        gather_scales(2)
+        load_x(1)
+        load_x(2)
         load_w1_head(1)
-        early[0, 1] = gather_words(held("head_words1", [P, HEAD], U32), head, 1)
-        gather_scales(HALF + 384, S)
-        load_x(X_CUTS[3])
+        gather_wide(1)
+        gather_scales(3)
+        load_x(3)
         load_w1_head(2)
-        load_x(X_CUTS[4])
+        load_x(4)
         load_w1_head(3)
-        move_last_plane(nc.sync)
+        move_last_plane()
         load_w1_head(4)
-        load_w1_rest(2)
-        move_planes(nc.sync, rest_planes, HALF, S)
-        load_w1_planes([nc.sync] * 4, "w1_planes1", 3, 6)
-        load_w1_rest(3)
-        load_w1_rest(4)
-        load_w1_rest(5)
+        load_w1_expert(2)
+        move_first_planes(nc.sync, 1)
+        load_w1_planes([nc.sync] * 4, 1)
+        for e in range(E // 2, E):
+            load_w1_expert(e)
         nc.sync.dma_start(out=w2[:].bitcast(I32), in_=w2_words[:, 0].rearrange("e p b -> p e b").bitcast(I32))
         w2_planes = load_weight_planes([nc.sync] * 4, "w2_planes", w2_scales)
         nc.sync.dma_start(pos1_t[:], pos1)
         nc.sync.dma_start(pos2_t[:], pos2)
         nc.sync.dma_start(out=gates[:], in_=gate.rearrange("r p t -> p r t"))
 
+        tile_words = {}
         h = {}
-        gathered = {}
 
-        def activate(j, acc, step):
+        def gather_pass(experts, a):
+            s0 = experts[0] * C
+            if s0 == 0 and a < WIDE_PASSES:
+                slot_words = head_words[a]
+            else:
+                slot_words = ring_tile([P, len(experts) * C], U32)
+                for e in experts:
+                    gather_words(slot_words[:, e * C - s0 : (e + 1) * C - s0], e * C, (e + 1) * C, a)
+            for j in range(experts[0] * TILES, (experts[-1] + 1) * TILES):
+                tile_words[j, a] = slot_words[:, j * P - s0 : (j + 1) * P - s0]
+
+        def first_matmul(acc, j, a):
+            if a == PASSES - 1:
+                token_plane = last_plane[:, j * P : (j + 1) * P]
+            else:
+                b, s0 = divmod(j * P, HALF)
+                token_plane = first_planes[b][:, a, s0 : s0 + P]
+            e = j // TILES
+            b, within = divmod(e, E // 2)
+            nc.tensor.matmul_mx(
+                out=acc[:],
+                lhsT=tile_words[j, a].bitcast(FP8X4),
+                lhsT_scale=token_plane,
+                rhs=w1_codes[e, a].bitcast(FP4X4),
+                rhs_scale=w1_planes[b][:, within * PASSES + a, :],
+                start=(a == 0),
+                stop=(a == PASSES - 1),
+            )
+
+        def activate(j, acc):
             h[j] = held("h%d" % j, [P, H], BF16)
+            step = 1 if j == LAST_TILE else 2
             for u in range(0, 2, step):
                 nc.scalar.activation(
                     out=h[j][:].rearrange("s (u p d) -> s u p d", u=2, d=2)[:, u : u + step],
@@ -205,38 +213,39 @@ def tile_moe_pkd_mlp_gelu_kernel(
                     func=GELU,
                 )
 
-        def first_layer(tiles, first_bank, order=None, first_words=None):
+        def first_layer(experts, first_bank):
+            tiles = range(experts[0] * TILES, (experts[-1] + 1) * TILES)
             accs = [bank_tile(first_bank + i, [P, H]) for i in range(len(tiles))]
-            words = {}
-            for i, a in order or [(i, a) for a in range(PASSES) for i in range(len(tiles))]:
-                if a not in words:
-                    if (tiles[0], a) in early:
-                        words[a] = early[tiles[0], a]
-                    elif a == 0 and first_words is not None:
-                        words[a] = gather_words(held(first_words, [P, len(tiles) * P], U32), tiles, a)
-                    else:
-                        words[a] = gather_words(ring_tile(len(tiles)), tiles, a)
-                j = tiles[i]
-                w1_codes, w1_plane = w1_operand(j // TILES, a)
-                nc.tensor.matmul_mx(
-                    out=accs[i][:],
-                    lhsT=words[a][:, i * P : (i + 1) * P].bitcast(FP8X4),
-                    lhsT_scale=token_plane(a, j),
-                    rhs=w1_codes,
-                    rhs_scale=w1_plane,
-                    start=(a == 0),
-                    stop=(a == PASSES - 1),
-                )
-                if a == PASSES - 1:
-                    activate(j, accs[i], 1 if j == S // P - 1 else 2)
+            for a in range(PASSES):
+                gather_pass(experts, a)
+                for j, acc in zip(tiles, accs):
+                    first_matmul(acc, j, a)
+                    if a == PASSES - 1:
+                        activate(j, acc)
+
+        def last_first_layer(first_bank):
+            e = E - 1
+            accs = [bank_tile(first_bank + i, [P, H]) for i in range(TILES)]
+            first_words = held(LATE_BUFFER, [P, C], U32)
+            gather_words(first_words[:], e * C, S, 0)
+            for i in range(TILES):
+                tile_words[e * TILES + i, 0] = first_words[:, i * P : (i + 1) * P]
+                first_matmul(accs[i], e * TILES + i, 0)
+            for i in range(TILES):
+                for a in range(1, PASSES):
+                    if i == 0:
+                        gather_pass([e], a)
+                    first_matmul(accs[i], e * TILES + i, a)
+                activate(e * TILES + i, accs[i])
 
         turned = {}
+        h_words = {}
 
-        def turn(tiles, b, copy):
-            n = len(tiles)
-            h_turned = held("h_turned%d" % tiles[0], [P, n * H], BF16)
+        def turn(group, b, copy):
+            n = len(group)
+            h_turned = held("h_turned%d" % group[0], [P, n * H], BF16)
             bank = bank_tile(b, [P, n, 2, P])
-            for i, j in enumerate(tiles):
+            for i, j in enumerate(group):
                 pairs = h[j][:].bitcast(F32)
                 for u in range(2):
                     nc.tensor.transpose(bank[:, i, u, :], pairs[:, u * P : (u + 1) * P], ident[:])
@@ -244,86 +253,78 @@ def tile_moe_pkd_mlp_gelu_kernel(
                 out=h_turned[:].bitcast(F32).rearrange("p (i s u) -> p i s u", i=n, u=2),
                 in_=bank[:].rearrange("p i u s -> p i s u"),
             )
-            turned[tiles[0]] = h_turned
+            turned[group] = h_turned
 
-        codes = {}
+        def slots_of(group):
+            return group[0] * P, (group[-1] + 1) * P
 
-        def quantize(tiles, h_plane):
-            s0, s1 = tiles[0] * P, (tiles[-1] + 1) * P
-            h_words = held("h_words%d" % tiles[0], [P, s1 - s0], U32)
-            nc.vector.quantize_mx(out=h_words[:].bitcast(FP8X4), scales=h_plane[:, s0:s1], in_=turned[tiles[0]][:])
-            codes[tiles[0]] = (h_words, h_plane[:, s0:s1])
+        def quantize(group):
+            s0, s1 = slots_of(group)
+            h_words[group] = held("h_words%d" % group[0], [P, s1 - s0], U32)
+            nc.vector.quantize_mx(out=h_words[group][:].bitcast(FP8X4), scales=h_plane[:, s0:s1], in_=turned[group][:])
 
         def second_layer(groups, b, copy):
-            s_first, s_last = groups[0][0] * P, (groups[-1][-1] + 1) * P
-            y_bank = bank_tile(b, [P, s_last - s_first])
-            for tiles in groups:
-                s0, s1 = tiles[0] * P, (tiles[-1] + 1) * P
+            first, last = slots_of(groups[0])[0], slots_of(groups[-1])[1]
+            y_bank = bank_tile(b, [P, last - first])
+            for group in groups:
+                s0, s1 = slots_of(group)
                 nc.tensor.matmul_mx(
-                    out=y_bank[:, s0 - s_first : s1 - s_first],
+                    out=y_bank[:, s0 - first : s1 - first],
                     lhsT=w2[:, s0 // C, :].bitcast(FP4X4),
                     lhsT_scale=w2_planes[:, s0 // C, :],
-                    rhs=codes[tiles[0]][0][:].bitcast(FP8X4),
-                    rhs_scale=codes[tiles[0]][1],
+                    rhs=h_words[group][:].bitcast(FP8X4),
+                    rhs_scale=h_plane[:, s0:s1],
                     start=True,
                     stop=True,
                 )
-            copy(out=y[:, s_first:s_last], in_=y_bank[:])
+            copy(out=y[:, first:last], in_=y_bank[:])
 
         on_scalar, on_vector = nc.scalar.copy, nc.vector.tensor_copy
-        warm_bank = bank_tile(7, [P, H])
-        for i in range(3):
-            w1_codes, w1_plane = w1_operand(0, 0)
-            nc.tensor.matmul_mx(
-                out=warm_bank[:],
-                lhsT=early[0, 0][:, 0:P].bitcast(FP8X4),
-                lhsT_scale=slot_scales[:, 0:P],
-                rhs=w1_codes,
-                rhs_scale=slot_scales[:, 0:H],
-                start=True,
-                stop=True,
-            )
-        first_layer(head, 0)
-        first_layer(expert[2], 4)
+        expert = [tuple(range(e * TILES, (e + 1) * TILES)) for e in range(E)]
+        next_to_last, last = [(j,) for j in expert[E - 1]]
+
+        first_layer([0, 1], 0)
+        first_layer([2], 4)
         turn(expert[0], 0, on_scalar)
         turn(expert[1], 1, on_scalar)
-        first_layer(expert[3], 6)
-        first_layer(expert[4], 2)
+        first_layer([3], 6)
+        first_layer([4], 2)
         turn(expert[2], 4, on_scalar)
         turn(expert[3], 5, on_scalar)
-        last_order = [(i, 0) for i in range(TILES)] + [(i, a) for i in range(TILES) for a in range(1, PASSES)]
-        first_layer(expert[5], 6, order=last_order, first_words="w1_rest3_0")
-        h_plane = held("w1_rest3_0", [P, S], U8)
+        last_first_layer(6)
+
+        h_plane = held(LATE_BUFFER, [P, S], U8)
         for e in range(4):
-            quantize(expert[e], h_plane)
+            quantize(expert[e])
         turn(expert[4], 6, on_vector)
-        turn([10], 0, on_vector)
+        turn(next_to_last, 0, on_vector)
         second_layer([expert[0], expert[1]], 1, on_scalar)
         second_layer([expert[2], expert[3]], 4, on_scalar)
-        quantize(expert[4], h_plane)
-        turn([11], 5, on_vector)
-        quantize([10], h_plane)
+        quantize(expert[4])
+        turn(last, 5, on_vector)
+        quantize(next_to_last)
         second_layer([expert[4]], 2, on_scalar)
-        quantize([11], h_plane)
-        second_layer([[10]], 3, on_scalar)
-        second_layer([[11]], 7, on_vector)
+        quantize(last)
+        second_layer([next_to_last], 3, on_scalar)
+        second_layer([last], 7, on_vector)
 
-
-        def fetch(r, pos_t, t0, t1):
-            picked = held("picked%d_%d" % (r, t0), [P, t1 - t0], F32)
-            nc.vector.tensor_tensor(picked[:], y[:].indirect(pos_t[:, t0 // 16 : t1 // 16]), gates[:, r, t0:t1], MULT)
+        def fetch(r, piece):
+            t0, t1 = TOKEN_CUTS[piece : piece + 2]
+            entries = (pos1_t, pos2_t)[r][:, t0 // 16 : t1 // 16]
+            picked = held("picked%d_%d" % (r, piece), [P, t1 - t0], F32)
+            nc.vector.tensor_tensor(picked[:], y[:].indirect(entries), gates[:, r, t0:t1], MULT)
             return picked
 
-        def add_and_store(queue, t0, t1, pair):
-            total = held("total%d" % t0, [P, t1 - t0], F32)
+        def add_and_store(queue, piece, pair):
+            t0, t1 = TOKEN_CUTS[piece : piece + 2]
+            total = held("total%d" % piece, [P, t1 - t0], F32)
             nc.vector.tensor_tensor(total[:], pair[0][:], pair[1][:], ADD)
             queue.dma_start(out=out[:, t0:t1], in_=total[:])
 
-        a0, a1, a2, a3 = 0, 384, 640, T
-        pair_a = [fetch(0, pos1_t, a0, a1), fetch(1, pos2_t, a0, a1)]
-        first_b = fetch(0, pos1_t, a1, a2)
-        add_and_store(nc.sync, a0, a1, pair_a)
-        pair_b = [first_b, fetch(1, pos2_t, a1, a2)]
-        pair_c = [fetch(0, pos1_t, a2, a3), fetch(1, pos2_t, a2, a3)]
-        add_and_store(nc.sync, a1, a2, pair_b)
-        add_and_store(nc.scalar, a2, a3, pair_c)
+        pair0 = [fetch(0, 0), fetch(1, 0)]
+        pair1 = [fetch(0, 1)]
+        add_and_store(nc.sync, 0, pair0)
+        pair1.append(fetch(1, 1))
+        pair2 = [fetch(0, 2), fetch(1, 2)]
+        add_and_store(nc.sync, 1, pair1)
+        add_and_store(nc.scalar, 2, pair2)

@@ -224,19 +224,14 @@ def tile_moe_pkd_mlp_gelu_kernel(
                         activate(j, acc)
 
         def last_first_layer(first_bank):
-            e = E - 1
-            accs = [bank_tile(first_bank + i, [P, H]) for i in range(TILES)]
-            first_words = held(LATE_BUFFER, [P, C], U32)
-            gather_words(first_words[:], e * C, S, 0)
-            for i in range(TILES):
-                tile_words[e * TILES + i, 0] = first_words[:, i * P : (i + 1) * P]
-                first_matmul(accs[i], e * TILES + i, 0)
-            for i in range(TILES):
-                for a in range(1, PASSES):
-                    if i == 0:
-                        gather_pass([e], a)
-                    first_matmul(accs[i], e * TILES + i, a)
-                activate(e * TILES + i, accs[i])
+            for i, j in enumerate(range((E - 1) * TILES, E * TILES)):
+                acc = bank_tile(first_bank + i, [P, H])
+                for a in range(PASSES):
+                    slot_words = held(LATE_BUFFER, [P, P], U32) if (i, a) == (0, 0) else ring_tile([P, P], U32)
+                    gather_words(slot_words[:], j * P, (j + 1) * P, a)
+                    tile_words[j, a] = slot_words[:]
+                    first_matmul(acc, j, a)
+                activate(j, acc)
 
         turned = {}
         h_words = {}

@@ -24,15 +24,15 @@ ADD = mybir.AluOpType.add
 ALIGN = 256
 TILES = C // P
 LAST_TILE = S // P - 1
-HEAD_EXPERTS = 2
+HEAD_EXPERTS = 3
 HEAD = HEAD_EXPERTS * C
 HALF = S // 2
 BYTE_GATHER = HALF // 2
 WIDE_PASSES = 2
 WORD_BUFS = 8
 SPLIT, WHOLE = ((0, 2), (2, PASSES)), ((0, PASSES),)
-W1_CUTS = {2: SPLIT, 3: SPLIT, 4: WHOLE, 5: WHOLE}
-LATE_BUFFER = "w1_expert3_0"
+W1_CUTS = {3: SPLIT, 4: WHOLE, 5: WHOLE}
+LATE_BUFFER = "w1_expert4_0"
 QUADS = (0, 2, 1, 3)
 LAST_ROWS = P - 16
 TOKEN_CUTS = (0, T // 2, T - P, T)
@@ -129,7 +129,8 @@ def tile_moe_pkd_mlp_gelu_kernel(
 
         def gather_wide(a):
             slot_words = held("head_words%d" % a, [P, HEAD], U32)
-            gather_words(slot_words[:], 0, HEAD, a)
+            for s0 in range(0, HEAD, BYTE_GATHER):
+                gather_words(slot_words[:, s0 : s0 + BYTE_GATHER], s0, s0 + BYTE_GATHER, a)
             head_words.append(slot_words)
 
         nc.vector.memset(scale_window[64:LAST_ROWS, :].bitcast(I32), 0)
@@ -160,7 +161,6 @@ def tile_moe_pkd_mlp_gelu_kernel(
         load_w1_head(3)
         move_last_plane()
         load_w1_head(4)
-        load_w1_expert(2)
         move_first_planes(nc.sync, 1)
         load_w1_planes([nc.sync] * 4, 1)
         for e in range(E // 2, E):
@@ -278,30 +278,29 @@ def tile_moe_pkd_mlp_gelu_kernel(
         expert = [tuple(range(e * TILES, (e + 1) * TILES)) for e in range(E)]
         next_to_last, last = [(j,) for j in expert[E - 1]]
 
-        first_layer([0, 1], 0)
-        first_layer([2], 4)
+        first_layer([0, 1, 2], 0)
         turn(expert[0], 0, on_scalar)
-        turn(expert[1], 1, on_scalar)
         first_layer([3], 6)
-        first_layer([4], 2)
-        turn(expert[2], 4, on_scalar)
-        turn(expert[3], 5, on_scalar)
-        last_first_layer(6)
+        first_layer([4], 1)
+        turn(expert[1], 6, on_scalar)
+        turn(expert[2], 7, on_scalar)
+        turn(expert[3], 0, on_vector)
+        last_first_layer(3)
 
         h_plane = held(LATE_BUFFER, [P, S], U8)
         for e in range(4):
             quantize(expert[e])
-        turn(expert[4], 6, on_vector)
-        turn(next_to_last, 0, on_vector)
+        turn(expert[4], 3, on_vector)
+        turn(next_to_last, 5, on_vector)
         second_layer([expert[0], expert[1]], 1, on_scalar)
-        second_layer([expert[2], expert[3]], 4, on_scalar)
+        second_layer([expert[2], expert[3]], 2, on_scalar)
         quantize(expert[4])
-        turn(last, 5, on_vector)
+        turn(last, 6, on_vector)
         quantize(next_to_last)
-        second_layer([expert[4]], 2, on_scalar)
+        second_layer([expert[4]], 7, on_scalar)
         quantize(last)
-        second_layer([next_to_last], 3, on_scalar)
-        second_layer([last], 7, on_vector)
+        second_layer([next_to_last], 0, on_scalar)
+        second_layer([last], 4, on_vector)
 
         def fetch(r, piece):
             t0, t1 = TOKEN_CUTS[piece : piece + 2]

@@ -70,19 +70,17 @@ def tile_moe_pkd_mlp_gelu_kernel(
         w2 = held("w2", [P, E, 2 * N], U8)
         ident = held("ident", [P, P], F32)
         y = held("y", [P, S], F32)
-        w1_planes = []
+        w1_planes = [held("w1_planes%d" % b, [P, E // 2 * PASSES, H], U8) for b in range(2)]
+        w2_planes = held("w2_planes", [P, E, N], U8)
         w1_codes = {}
 
-        def load_weight_planes(queues, name, scales):
-            rows = scales.rearrange("e s (q r) n -> r q (e s) n", r=4)
-            planes = held(name, [P, rows.shape[2], rows.shape[3]], U8)
-            for r, queue in enumerate(queues):
-                queue.dma_start(out=planes[r:P:32].bitcast(I32), in_=rows[r].bitcast(I32))
-            return planes
+        def load_planes(planes, scales, rows):
+            by_row = scales.rearrange("e s (q r) n -> r q (e s) n", r=4)
+            for r in rows:
+                nc.sync.dma_start(out=planes[r:P:32].bitcast(I32), in_=by_row[r].bitcast(I32))
 
-        def load_w1_planes(queues, b):
-            scales = w1_scales[b * E // 2 : (b + 1) * E // 2]
-            w1_planes.append(load_weight_planes(queues, "w1_planes%d" % b, scales))
+        def load_w1_planes(b, rows):
+            load_planes(w1_planes[b], w1_scales[b * E // 2 : (b + 1) * E // 2], rows)
 
         def load_x(a):
             nc.sync.dma_start(out=word_windows[a][:], in_=x_words[a].rearrange("p t r -> p (t r)").bitcast(I32))
@@ -144,13 +142,14 @@ def tile_moe_pkd_mlp_gelu_kernel(
         gather_scales(1)
         move_first_planes(nc.scalar, 0)
         load_x(0)
-        load_w1_planes([nc.gpsimd, nc.gpsimd, nc.sync, nc.sync], 0)
+        load_w1_planes(0, (0, 1))
         nc.vector.memset(ident[:], 0.0)
         make_identity(nc, ident[:], nomemset=True)
         load_w1_head(0)
         gather_wide(0)
         gather_scales(2)
         load_x(1)
+        load_w1_planes(0, (2, 3))
         load_x(2)
         load_w1_head(1)
         gather_wide(1)
@@ -162,11 +161,11 @@ def tile_moe_pkd_mlp_gelu_kernel(
         move_last_plane()
         load_w1_head(4)
         move_first_planes(nc.sync, 1)
-        load_w1_planes([nc.sync] * 4, 1)
+        load_w1_planes(1, range(4))
         for e in range(E // 2, E):
             load_w1_expert(e)
         nc.sync.dma_start(out=w2[:].bitcast(I32), in_=w2_words[:, 0].rearrange("e p b -> p e b").bitcast(I32))
-        w2_planes = load_weight_planes([nc.sync] * 4, "w2_planes", w2_scales)
+        load_planes(w2_planes, w2_scales, range(4))
         nc.sync.dma_start(pos1_t[:], pos1)
         nc.sync.dma_start(pos2_t[:], pos2)
         nc.sync.dma_start(out=gates[:], in_=gate.rearrange("r p t -> p r t"))

@@ -27,12 +27,13 @@ LAST_TILE = S // P - 1
 HEAD_EXPERTS = 3
 HEAD = HEAD_EXPERTS * C
 HALF = S // 2
-BYTE_GATHER = HALF // 2
+WIDE_GATHER = HALF // 2
 WIDE_PASSES = 2
-WORD_BUFS = 8
+WORD_BUFS = 10
 SPLIT, WHOLE = ((0, 2), (2, PASSES)), ((0, PASSES),)
-W1_CUTS = {3: SPLIT, 4: WHOLE, 5: WHOLE}
-LATE_BUFFER = "w1_expert4_0"
+W1_CUTS = {3: SPLIT, 4: SPLIT, 5: WHOLE}
+PLANE_SETS = ((0, 3), (3, 4), (4, 6))
+IDENT_BUFFER = "w1_expert4_0"
 QUADS = (0, 2, 1, 3)
 LAST_ROWS = P - 16
 TOKEN_CUTS = (0, T // 2, T - P, T)
@@ -64,13 +65,15 @@ def tile_moe_pkd_mlp_gelu_kernel(
         scale_window = held("scale_window", [P, T], U8)
         word_windows = [held("word_window%d" % a, [P, T], I32) for a in range(PASSES)]
         slot_scales = held("slot_scales", [P, S], U8)
-        first_planes = [held("first_planes%d" % b, [P, 4, HALF], U8) for b in range(2)]
+        first_planes = [ring_tile([P, 4, HALF], U8), held("first_planes1", [P, 4, HALF], U8)]
         last_plane = held("last_plane", [P, S], U8)
         gates = held("gates", [P, 2, T], F32)
         w2 = held("w2", [P, E, 2 * N], U8)
-        ident = held("ident", [P, P], F32)
+        h_plane = held("h_plane", [P, S], U8)
+        early_ident = held("early_ident", [P, P], F32)
         y = held("y", [P, S], F32)
-        w1_planes = [held("w1_planes%d" % b, [P, E // 2 * PASSES, H], U8) for b in range(2)]
+        w1_planes = [ring_tile([P, HEAD_EXPERTS * PASSES, H], U8)]
+        w1_planes.extend(held("w1_planes%d" % e0, [P, (e1 - e0) * PASSES, H], U8) for e0, e1 in PLANE_SETS[1:])
         w2_planes = held("w2_planes", [P, E, N], U8)
         w1_codes = {}
 
@@ -80,7 +83,8 @@ def tile_moe_pkd_mlp_gelu_kernel(
                 nc.sync.dma_start(out=planes[r:P:32].bitcast(I32), in_=by_row[r].bitcast(I32))
 
         def load_w1_planes(b, rows):
-            load_planes(w1_planes[b], w1_scales[b * E // 2 : (b + 1) * E // 2], rows)
+            e0, e1 = PLANE_SETS[b]
+            load_planes(w1_planes[b], w1_scales[e0:e1], rows)
 
         def load_x(a):
             nc.sync.dma_start(out=word_windows[a][:], in_=x_words[a].rearrange("p t r -> p (t r)").bitcast(I32))
@@ -109,14 +113,14 @@ def tile_moe_pkd_mlp_gelu_kernel(
                 )
 
         def move_last_plane():
-            for q in QUADS:
+            for r in range(4):
                 nc.sync.dma_start(
-                    out=last_plane[32 * q : 32 * q + 4, :].bitcast(I32),
-                    in_=slot_scales[LAST_ROWS + 4 * q : LAST_ROWS + 4 * q + 4, :].bitcast(I32),
+                    out=last_plane[r:P:32, :].bitcast(I32),
+                    in_=slot_scales[LAST_ROWS + r : P : 4, :].bitcast(I32),
                 )
 
         def gather_scales(g):
-            s0, s1 = g * BYTE_GATHER, (g + 1) * BYTE_GATHER
+            s0, s1 = g * WIDE_GATHER, (g + 1) * WIDE_GATHER
             nc.vector.tensor_copy(slot_scales[:, s0:s1], scale_window[:].indirect(offs_t[:, s0 // 16 : s1 // 16]))
 
         def gather_words(slot_words, s0, s1, a):
@@ -127,8 +131,8 @@ def tile_moe_pkd_mlp_gelu_kernel(
 
         def gather_wide(a):
             slot_words = held("head_words%d" % a, [P, HEAD], U32)
-            for s0 in range(0, HEAD, BYTE_GATHER):
-                gather_words(slot_words[:, s0 : s0 + BYTE_GATHER], s0, s0 + BYTE_GATHER, a)
+            for s0 in range(0, HEAD, WIDE_GATHER):
+                gather_words(slot_words[:, s0 : s0 + WIDE_GATHER], s0, s0 + WIDE_GATHER, a)
             head_words.append(slot_words)
 
         nc.vector.memset(scale_window[64:LAST_ROWS, :].bitcast(I32), 0)
@@ -143,13 +147,13 @@ def tile_moe_pkd_mlp_gelu_kernel(
         move_first_planes(nc.scalar, 0)
         load_x(0)
         load_w1_planes(0, (0, 1))
-        nc.vector.memset(ident[:], 0.0)
-        make_identity(nc, ident[:], nomemset=True)
+        nc.vector.memset(early_ident[:], 0.0)
+        make_identity(nc, early_ident[:], nomemset=True)
         load_w1_head(0)
         gather_wide(0)
         gather_scales(2)
-        load_x(1)
         load_w1_planes(0, (2, 3))
+        load_x(1)
         load_x(2)
         load_w1_head(1)
         gather_wide(1)
@@ -162,8 +166,10 @@ def tile_moe_pkd_mlp_gelu_kernel(
         load_w1_head(4)
         move_first_planes(nc.sync, 1)
         load_w1_planes(1, range(4))
-        for e in range(E // 2, E):
-            load_w1_expert(e)
+        load_w1_expert(3)
+        load_w1_planes(2, range(4))
+        load_w1_expert(4)
+        load_w1_expert(5)
         nc.sync.dma_start(out=w2[:].bitcast(I32), in_=w2_words[:, 0].rearrange("e p b -> p e b").bitcast(I32))
         load_planes(w2_planes, w2_scales, range(4))
         nc.sync.dma_start(pos1_t[:], pos1)
@@ -191,7 +197,8 @@ def tile_moe_pkd_mlp_gelu_kernel(
                 b, s0 = divmod(j * P, HALF)
                 token_plane = first_planes[b][:, a, s0 : s0 + P]
             e = j // TILES
-            b, within = divmod(e, E // 2)
+            b = sum(e >= e1 for e0, e1 in PLANE_SETS)
+            within = e - PLANE_SETS[b][0]
             nc.tensor.matmul_mx(
                 out=acc[:],
                 lhsT=tile_words[j, a].bitcast(FP8X4),
@@ -226,7 +233,7 @@ def tile_moe_pkd_mlp_gelu_kernel(
             for i, j in enumerate(range((E - 1) * TILES, E * TILES)):
                 acc = bank_tile(first_bank + i, [P, H])
                 for a in range(PASSES):
-                    slot_words = held(LATE_BUFFER, [P, P], U32) if (i, a) == (0, 0) else ring_tile([P, P], U32)
+                    slot_words = ring_tile([P, P], U32)
                     gather_words(slot_words[:], j * P, (j + 1) * P, a)
                     tile_words[j, a] = slot_words[:]
                     first_matmul(acc, j, a)
@@ -278,28 +285,29 @@ def tile_moe_pkd_mlp_gelu_kernel(
         next_to_last, last = [(j,) for j in expert[E - 1]]
 
         first_layer([0, 1, 2], 0)
-        turn(expert[0], 0, on_scalar)
         first_layer([3], 6)
         first_layer([4], 1)
-        turn(expert[1], 6, on_scalar)
-        turn(expert[2], 7, on_scalar)
-        turn(expert[3], 0, on_vector)
-        last_first_layer(3)
+        ident = held(IDENT_BUFFER, [P, P], F32)
+        nc.scalar.copy(out=ident[:], in_=early_ident[:])
+        turn(expert[0], 0, on_scalar)
+        turn(expert[1], 3, on_scalar)
+        turn(expert[2], 6, on_scalar)
+        turn(expert[3], 7, on_scalar)
+        last_first_layer(4)
 
-        h_plane = held(LATE_BUFFER, [P, S], U8)
         for e in range(4):
             quantize(expert[e])
-        turn(expert[4], 3, on_vector)
-        turn(next_to_last, 5, on_vector)
+        turn(expert[4], 4, on_vector)
+        turn(next_to_last, 0, on_vector)
         second_layer([expert[0], expert[1]], 1, on_scalar)
         second_layer([expert[2], expert[3]], 2, on_scalar)
         quantize(expert[4])
-        turn(last, 6, on_vector)
+        turn(last, 3, on_vector)
         quantize(next_to_last)
-        second_layer([expert[4]], 7, on_scalar)
+        second_layer([expert[4]], 6, on_scalar)
         quantize(last)
-        second_layer([next_to_last], 0, on_scalar)
-        second_layer([last], 4, on_vector)
+        second_layer([next_to_last], 7, on_scalar)
+        second_layer([last], 5, on_vector)
 
         def fetch(r, piece):
             t0, t1 = TOKEN_CUTS[piece : piece + 2]

@@ -18,6 +18,7 @@ U8 = mybir.dt.uint8
 FP8X4 = mybir.dt.float8_e4m3fn_x4
 FP4X4 = mybir.dt.float4_e2m1fn_x4
 GELU = mybir.ActivationFunctionType.Gelu_apprx_tanh
+COPY = mybir.ActivationFunctionType.Copy
 MULT = mybir.AluOpType.mult
 ADD = mybir.AluOpType.add
 
@@ -309,23 +310,47 @@ def tile_moe_pkd_mlp_gelu_kernel(
         second_layer([next_to_last], 7, on_scalar)
         second_layer([last], 5, on_vector)
 
-        def fetch(r, piece):
-            t0, t1 = TOKEN_CUTS[piece : piece + 2]
-            entries = (pos1_t, pos2_t)[r][:, t0 // 16 : t1 // 16]
-            picked = held("picked%d_%d" % (r, piece), [P, t1 - t0], F32)
-            nc.vector.tensor_tensor(picked[:], y[:].indirect(entries), gates[:, r, t0:t1], MULT)
-            return picked
+        pos_t = (pos1_t, pos2_t)
 
-        def add_and_store(queue, piece, pair):
+        def entries_of(r, piece):
+            t0, t1 = TOKEN_CUTS[piece : piece + 2]
+            return y[:].indirect(pos_t[r][:, t0 // 16 : t1 // 16])
+
+        def gate_of(r, piece):
+            return gates[:, r, TOKEN_CUTS[piece] : TOKEN_CUTS[piece + 1]]
+
+        def piece_tile(name, r, piece):
+            return held("%s%d_%d" % (name, r, piece), [P, TOKEN_CUTS[piece + 1] - TOKEN_CUTS[piece]], F32)
+
+        picked = {}
+        weighted = {}
+
+        def fetch_on_scalar(r, piece):
+            picked[r, piece] = piece_tile("picked", r, piece)
+            nc.scalar.activation(picked[r, piece][:], entries_of(r, piece), COPY)
+
+        def fetch_on_vector(r, piece):
+            weighted[r, piece] = piece_tile("weighted", r, piece)
+            nc.vector.tensor_tensor(weighted[r, piece][:], entries_of(r, piece), gate_of(r, piece), MULT)
+
+        def weigh(r, piece):
+            weighted[r, piece] = piece_tile("weighted", r, piece)
+            nc.vector.tensor_tensor(weighted[r, piece][:], picked[r, piece][:], gate_of(r, piece), MULT)
+
+        def add_and_store(queue, piece):
             t0, t1 = TOKEN_CUTS[piece : piece + 2]
             total = held("total%d" % piece, [P, t1 - t0], F32)
-            nc.vector.tensor_tensor(total[:], pair[0][:], pair[1][:], ADD)
+            nc.vector.tensor_tensor(total[:], weighted[0, piece][:], weighted[1, piece][:], ADD)
             queue.dma_start(out=out[:, t0:t1], in_=total[:])
 
-        pair0 = [fetch(0, 0), fetch(1, 0)]
-        pair1 = [fetch(0, 1)]
-        add_and_store(nc.sync, 0, pair0)
-        pair1.append(fetch(1, 1))
-        pair2 = [fetch(0, 2), fetch(1, 2)]
-        add_and_store(nc.sync, 1, pair1)
-        add_and_store(nc.scalar, 2, pair2)
+        fetch_on_vector(0, 0)
+        for r, piece in ((1, 0), (0, 1), (1, 1), (0, 2), (1, 2)):
+            fetch_on_scalar(r, piece)
+        weigh(1, 0)
+        weigh(0, 1)
+        add_and_store(nc.sync, 0)
+        weigh(1, 1)
+        weigh(0, 2)
+        add_and_store(nc.sync, 1)
+        weigh(1, 2)
+        add_and_store(nc.scalar, 2)

@@ -24,17 +24,18 @@ ADD = mybir.AluOpType.add
 
 ALIGN = 256
 TILES = C // P
-LAST_TILE = S // P - 1
 HEAD_EXPERTS = 3
 HEAD = HEAD_EXPERTS * C
 HALF = S // 2
 WIDE_GATHER = HALF // 2
 WIDE_PASSES = 2
+SHIFT = 32
 WORD_BUFS = 10
 SPLIT, WHOLE = ((0, 2), (2, PASSES)), ((0, PASSES),)
 W1_CUTS = {3: SPLIT, 4: SPLIT, 5: WHOLE}
 PLANE_SETS = ((0, 3), (3, 4), (4, 6))
 IDENT_BUFFER = "w1_expert4_0"
+LAST_BANKS = ((4,), (6, 5))
 QUADS = (0, 2, 1, 3)
 LAST_ROWS = P - 16
 TOKEN_CUTS = (0, T // 2, T - P, T)
@@ -131,7 +132,7 @@ def tile_moe_pkd_mlp_gelu_kernel(
         head_words = []
 
         def gather_wide(a):
-            slot_words = held("head_words%d" % a, [P, HEAD], U32)
+            slot_words = held("head_words%d" % a, [P, SHIFT + HEAD], U32)[:, SHIFT:]
             for s0 in range(0, HEAD, WIDE_GATHER):
                 gather_words(slot_words[:, s0 : s0 + WIDE_GATHER], s0, s0 + WIDE_GATHER, a)
             head_words.append(slot_words)
@@ -185,13 +186,13 @@ def tile_moe_pkd_mlp_gelu_kernel(
             if s0 == 0 and a < WIDE_PASSES:
                 slot_words = head_words[a]
             else:
-                slot_words = ring_tile([P, len(experts) * C], U32)
+                slot_words = ring_tile([P, SHIFT + len(experts) * C], U32)[:, SHIFT:]
                 for e in experts:
                     gather_words(slot_words[:, e * C - s0 : (e + 1) * C - s0], e * C, (e + 1) * C, a)
             for j in range(experts[0] * TILES, (experts[-1] + 1) * TILES):
                 tile_words[j, a] = slot_words[:, j * P - s0 : (j + 1) * P - s0]
 
-        def first_matmul(acc, j, a):
+        def first_matmul(acc, j, a, i0=0, i1=H):
             if a == PASSES - 1:
                 token_plane = last_plane[:, j * P : (j + 1) * P]
             else:
@@ -204,21 +205,20 @@ def tile_moe_pkd_mlp_gelu_kernel(
                 out=acc[:],
                 lhsT=tile_words[j, a].bitcast(FP8X4),
                 lhsT_scale=token_plane,
-                rhs=w1_codes[e, a].bitcast(FP4X4),
-                rhs_scale=w1_planes[b][:, within * PASSES + a, :],
+                rhs=w1_codes[e, a][:, 2 * i0 : 2 * i1].bitcast(FP4X4),
+                rhs_scale=w1_planes[b][:, within * PASSES + a, i0:i1],
                 start=(a == 0),
                 stop=(a == PASSES - 1),
             )
 
-        def activate(j, acc):
-            h[j] = held("h%d" % j, [P, H], BF16)
-            step = 1 if j == LAST_TILE else 2
-            for u in range(0, 2, step):
-                nc.scalar.activation(
-                    out=h[j][:].rearrange("s (u p d) -> s u p d", u=2, d=2)[:, u : u + step],
-                    in_=acc[:].rearrange("s (p u d) -> s u p d", u=2, d=2)[:, u : u + step],
-                    func=GELU,
-                )
+        def activate(j, acc, i0=0, i1=H):
+            if i0 == 0:
+                h[j] = held("h%d" % j, [P, H], BF16)
+            nc.scalar.activation(
+                out=h[j][:].rearrange("s (u p d) -> s u p d", u=2, d=2)[:, :, i0 // 4 : i1 // 4],
+                in_=acc[:].rearrange("s (p u d) -> s u p d", u=2, d=2),
+                func=GELU,
+            )
 
         def first_layer(experts, first_bank):
             tiles = range(experts[0] * TILES, (experts[-1] + 1) * TILES)
@@ -230,32 +230,45 @@ def tile_moe_pkd_mlp_gelu_kernel(
                     if a == PASSES - 1:
                         activate(j, acc)
 
-        def last_first_layer(first_bank):
-            for i, j in enumerate(range((E - 1) * TILES, E * TILES)):
-                acc = bank_tile(first_bank + i, [P, H])
-                for a in range(PASSES):
-                    slot_words = ring_tile([P, P], U32)
-                    gather_words(slot_words[:], j * P, (j + 1) * P, a)
-                    tile_words[j, a] = slot_words[:]
-                    first_matmul(acc, j, a)
-                activate(j, acc)
+        def last_first_layer():
+            for j, tile_banks in zip(range((E - 1) * TILES, E * TILES), LAST_BANKS):
+                width = H // len(tile_banks)
+                for g, b in enumerate(tile_banks):
+                    acc = bank_tile(b, [P, width])
+                    for a in range(PASSES):
+                        if g == 0:
+                            slot_words = ring_tile([P, SHIFT + P], U32)[:, SHIFT:]
+                            gather_words(slot_words, j * P, (j + 1) * P, a)
+                            tile_words[j, a] = slot_words
+                        first_matmul(acc, j, a, g * width, (g + 1) * width)
+                    activate(j, acc, g * width, (g + 1) * width)
 
         turned = {}
         h_words = {}
 
-        def turn(group, b, copy):
+        turned_banks = {}
+
+        def transpose(group, b):
             n = len(group)
-            h_turned = held("h_turned%d" % group[0], [P, n * H], BF16)
             bank = bank_tile(b, [P, n, 2, P])
+            turned_banks[group] = bank
             for i, j in enumerate(group):
                 pairs = h[j][:].bitcast(F32)
                 for u in range(2):
                     nc.tensor.transpose(bank[:, i, u, :], pairs[:, u * P : (u + 1) * P], ident[:])
+
+        def copy_turned(group, copy):
+            n = len(group)
+            h_turned = held("h_turned%d" % group[0], [P, n * H], BF16)
             copy(
                 out=h_turned[:].bitcast(F32).rearrange("p (i s u) -> p i s u", i=n, u=2),
-                in_=bank[:].rearrange("p i u s -> p i s u"),
+                in_=turned_banks[group][:].rearrange("p i u s -> p i s u"),
             )
             turned[group] = h_turned
+
+        def turn(group, b, copy):
+            transpose(group, b)
+            copy_turned(group, copy)
 
         def slots_of(group):
             return group[0] * P, (group[-1] + 1) * P
@@ -294,21 +307,20 @@ def tile_moe_pkd_mlp_gelu_kernel(
         turn(expert[1], 3, on_scalar)
         turn(expert[2], 6, on_scalar)
         turn(expert[3], 7, on_scalar)
-        last_first_layer(4)
+        transpose(expert[4], 1)
+        last_first_layer()
+        copy_turned(expert[4], on_vector)
 
-        for e in range(4):
+        for e in range(5):
             quantize(expert[e])
-        turn(expert[4], 4, on_vector)
         turn(next_to_last, 0, on_vector)
-        second_layer([expert[0], expert[1]], 1, on_scalar)
-        second_layer([expert[2], expert[3]], 2, on_scalar)
-        quantize(expert[4])
-        turn(last, 3, on_vector)
+        second_layer([expert[0], expert[1]], 6, on_vector)
         quantize(next_to_last)
-        second_layer([expert[4]], 6, on_scalar)
+        turn(last, 3, on_scalar)
+        second_layer([expert[2], expert[3]], 5, on_scalar)
         quantize(last)
-        second_layer([next_to_last], 7, on_scalar)
-        second_layer([last], 5, on_vector)
+        second_layer([expert[4]], 0, on_scalar)
+        second_layer([next_to_last, last], 4, on_scalar)
 
         pos_t = (pos1_t, pos2_t)
 
@@ -351,6 +363,6 @@ def tile_moe_pkd_mlp_gelu_kernel(
         add_and_store(nc.sync, 0)
         weigh(1, 1)
         weigh(0, 2)
-        add_and_store(nc.sync, 1)
         weigh(1, 2)
+        add_and_store(nc.sync, 1)
         add_and_store(nc.scalar, 2)

@@ -220,15 +220,18 @@ def tile_moe_pkd_mlp_gelu_kernel(
                 func=GELU,
             )
 
-        def first_layer(experts, first_bank):
+        accs = {}
+
+        def first_layer(experts, first_bank, passes=range(PASSES), late=()):
             tiles = range(experts[0] * TILES, (experts[-1] + 1) * TILES)
-            accs = [bank_tile(first_bank + i, [P, H]) for i in range(len(tiles))]
-            for a in range(PASSES):
+            for a in passes:
                 gather_pass(experts, a)
-                for j, acc in zip(tiles, accs):
-                    first_matmul(acc, j, a)
-                    if a == PASSES - 1:
-                        activate(j, acc)
+                for i, j in enumerate(tiles):
+                    if a == 0:
+                        accs[j] = bank_tile(first_bank + i, [P, H])
+                    first_matmul(accs[j], j, a)
+                    if a == PASSES - 1 and j not in late:
+                        activate(j, accs[j])
 
         def last_first_layer():
             for j, tile_banks in zip(range((E - 1) * TILES, E * TILES), LAST_BANKS):
@@ -248,14 +251,14 @@ def tile_moe_pkd_mlp_gelu_kernel(
 
         turned_banks = {}
 
-        def transpose(group, b):
+        def transpose(group, b, identity=None):
             n = len(group)
             bank = bank_tile(b, [P, n, 2, P])
             turned_banks[group] = bank
             for i, j in enumerate(group):
                 pairs = h[j][:].bitcast(F32)
                 for u in range(2):
-                    nc.tensor.transpose(bank[:, i, u, :], pairs[:, u * P : (u + 1) * P], ident[:])
+                    nc.tensor.transpose(bank[:, i, u, :], pairs[:, u * P : (u + 1) * P], (ident if identity is None else identity)[:])
 
         def copy_turned(group, copy):
             n = len(group)
@@ -298,29 +301,35 @@ def tile_moe_pkd_mlp_gelu_kernel(
         expert = [tuple(range(e * TILES, (e + 1) * TILES)) for e in range(E)]
         next_to_last, last = [(j,) for j in expert[E - 1]]
 
-        first_layer([0, 1, 2], 0)
-        first_layer([3], 6)
-        first_layer([4], 1)
+        first_layer([0, 1, 2], 0, late=expert[2])
+        first_layer([3], 6, range(2))
+        ident = held("w1_expert3_0", [P, P], F32)
+        nc.scalar.copy(out=ident[:], in_=early_ident[:])
+        for j in expert[2]:
+            activate(j, accs[j])
+        first_layer([3], 6, range(2, PASSES))
+        for e in range(2):
+            transpose(expert[e], e, ident)
+            copy_turned(expert[e], on_scalar)
+        first_layer([4], 2)
         ident = held(IDENT_BUFFER, [P, P], F32)
         nc.scalar.copy(out=ident[:], in_=early_ident[:])
-        turn(expert[0], 0, on_scalar)
-        turn(expert[1], 3, on_scalar)
         turn(expert[2], 6, on_scalar)
         turn(expert[3], 7, on_scalar)
-        transpose(expert[4], 1)
         last_first_layer()
-        copy_turned(expert[4], on_vector)
 
-        for e in range(5):
+        for e in range(4):
             quantize(expert[e])
-        turn(next_to_last, 0, on_vector)
-        second_layer([expert[0], expert[1]], 6, on_vector)
-        quantize(next_to_last)
+        turn(expert[4], 4, on_vector)
+        turn(next_to_last, 0, on_scalar)
         turn(last, 3, on_scalar)
-        second_layer([expert[2], expert[3]], 5, on_scalar)
+        quantize(expert[4])
+        second_layer([expert[2], expert[3]], 6, on_scalar)
+        quantize(next_to_last)
+        second_layer([expert[0], expert[1]], 5, on_scalar)
         quantize(last)
-        second_layer([expert[4]], 0, on_scalar)
-        second_layer([next_to_last, last], 4, on_scalar)
+        second_layer([expert[4]], 4, on_vector)
+        second_layer([next_to_last, last], 1, on_vector)
 
         pos_t = (pos1_t, pos2_t)
 

@@ -29,12 +29,10 @@ HEAD = HEAD_EXPERTS * C
 HALF = S // 2
 WIDE_GATHER = HALF // 2
 WIDE_PASSES = 2
-SHIFT = 32
 WORD_BUFS = 10
 SPLIT, WHOLE = ((0, 2), (2, PASSES)), ((0, PASSES),)
 W1_CUTS = {3: SPLIT, 4: SPLIT, 5: WHOLE}
 PLANE_SETS = ((0, 3), (3, 4), (4, 6))
-IDENT_BUFFER = "w1_expert4_0"
 LAST_BANKS = ((4,), (6, 5))
 QUADS = (0, 2, 1, 3)
 LAST_ROWS = P - 16
@@ -84,9 +82,9 @@ def tile_moe_pkd_mlp_gelu_kernel(
             for r in rows:
                 nc.sync.dma_start(out=planes[r:P:32].bitcast(I32), in_=by_row[r].bitcast(I32))
 
-        def load_w1_planes(b, rows):
-            e0, e1 = PLANE_SETS[b]
-            load_planes(w1_planes[b], w1_scales[e0:e1], rows)
+        def load_w1_planes(plane_set, rows):
+            e0, e1 = PLANE_SETS[plane_set]
+            load_planes(w1_planes[plane_set], w1_scales[e0:e1], rows)
 
         def load_x(a):
             nc.sync.dma_start(out=word_windows[a][:], in_=x_words[a].rearrange("p t r -> p (t r)").bitcast(I32))
@@ -107,11 +105,11 @@ def tile_moe_pkd_mlp_gelu_kernel(
                 for a in range(a0, a1):
                     w1_codes[e, a] = piece[:, a - a0, :]
 
-        def move_first_planes(queue, b):
+        def move_first_planes(queue, half):
             for q in QUADS:
                 queue.dma_start(
-                    out=first_planes[b][32 * q : 32 * q + 4].bitcast(I32),
-                    in_=slot_scales[16 * q : 16 * q + 16, b * HALF : (b + 1) * HALF].bitcast(I32),
+                    out=first_planes[half][32 * q : 32 * q + 4].bitcast(I32),
+                    in_=slot_scales[16 * q : 16 * q + 16, half * HALF : (half + 1) * HALF].bitcast(I32),
                 )
 
         def move_last_plane():
@@ -132,7 +130,7 @@ def tile_moe_pkd_mlp_gelu_kernel(
         head_words = []
 
         def gather_wide(a):
-            slot_words = held("head_words%d" % a, [P, SHIFT + HEAD], U32)[:, SHIFT:]
+            slot_words = held("head_words%d" % a, [P, HEAD], U32)
             for s0 in range(0, HEAD, WIDE_GATHER):
                 gather_words(slot_words[:, s0 : s0 + WIDE_GATHER], s0, s0 + WIDE_GATHER, a)
             head_words.append(slot_words)
@@ -186,7 +184,7 @@ def tile_moe_pkd_mlp_gelu_kernel(
             if s0 == 0 and a < WIDE_PASSES:
                 slot_words = head_words[a]
             else:
-                slot_words = ring_tile([P, SHIFT + len(experts) * C], U32)[:, SHIFT:]
+                slot_words = ring_tile([P, len(experts) * C], U32)
                 for e in experts:
                     gather_words(slot_words[:, e * C - s0 : (e + 1) * C - s0], e * C, (e + 1) * C, a)
             for j in range(experts[0] * TILES, (experts[-1] + 1) * TILES):
@@ -196,17 +194,17 @@ def tile_moe_pkd_mlp_gelu_kernel(
             if a == PASSES - 1:
                 token_plane = last_plane[:, j * P : (j + 1) * P]
             else:
-                b, s0 = divmod(j * P, HALF)
-                token_plane = first_planes[b][:, a, s0 : s0 + P]
+                half, s0 = divmod(j * P, HALF)
+                token_plane = first_planes[half][:, a, s0 : s0 + P]
             e = j // TILES
-            b = sum(e >= e1 for e0, e1 in PLANE_SETS)
-            within = e - PLANE_SETS[b][0]
+            plane_set = sum(e >= e1 for e0, e1 in PLANE_SETS)
+            within = e - PLANE_SETS[plane_set][0]
             nc.tensor.matmul_mx(
                 out=acc[:],
                 lhsT=tile_words[j, a].bitcast(FP8X4),
                 lhsT_scale=token_plane,
                 rhs=w1_codes[e, a][:, 2 * i0 : 2 * i1].bitcast(FP4X4),
-                rhs_scale=w1_planes[b][:, within * PASSES + a, i0:i1],
+                rhs_scale=w1_planes[plane_set][:, within * PASSES + a, i0:i1],
                 start=(a == 0),
                 stop=(a == PASSES - 1),
             )
@@ -240,38 +238,33 @@ def tile_moe_pkd_mlp_gelu_kernel(
                     acc = bank_tile(b, [P, width])
                     for a in range(PASSES):
                         if g == 0:
-                            slot_words = ring_tile([P, SHIFT + P], U32)[:, SHIFT:]
-                            gather_words(slot_words, j * P, (j + 1) * P, a)
-                            tile_words[j, a] = slot_words
+                            slot_words = ring_tile([P, P], U32)
+                            gather_words(slot_words[:], j * P, (j + 1) * P, a)
+                            tile_words[j, a] = slot_words[:]
                         first_matmul(acc, j, a, g * width, (g + 1) * width)
                     activate(j, acc, g * width, (g + 1) * width)
 
         turned = {}
         h_words = {}
 
-        turned_banks = {}
+        def late_identity(e):
+            ident = held("w1_expert%d_0" % e, [P, P], F32)
+            nc.scalar.copy(out=ident[:], in_=early_ident[:])
+            return ident
 
-        def transpose(group, b, identity=None):
+        def turn(group, b, ident, copy):
             n = len(group)
             bank = bank_tile(b, [P, n, 2, P])
-            turned_banks[group] = bank
             for i, j in enumerate(group):
                 pairs = h[j][:].bitcast(F32)
                 for u in range(2):
-                    nc.tensor.transpose(bank[:, i, u, :], pairs[:, u * P : (u + 1) * P], (ident if identity is None else identity)[:])
-
-        def copy_turned(group, copy):
-            n = len(group)
+                    nc.tensor.transpose(bank[:, i, u, :], pairs[:, u * P : (u + 1) * P], ident[:])
             h_turned = held("h_turned%d" % group[0], [P, n * H], BF16)
             copy(
                 out=h_turned[:].bitcast(F32).rearrange("p (i s u) -> p i s u", i=n, u=2),
-                in_=turned_banks[group][:].rearrange("p i u s -> p i s u"),
+                in_=bank[:].rearrange("p i u s -> p i s u"),
             )
             turned[group] = h_turned
-
-        def turn(group, b, copy):
-            transpose(group, b)
-            copy_turned(group, copy)
 
         def slots_of(group):
             return group[0] * P, (group[-1] + 1) * P
@@ -282,8 +275,8 @@ def tile_moe_pkd_mlp_gelu_kernel(
             nc.vector.quantize_mx(out=h_words[group][:].bitcast(FP8X4), scales=h_plane[:, s0:s1], in_=turned[group][:])
 
         def second_layer(groups, b, copy):
-            first, last = slots_of(groups[0])[0], slots_of(groups[-1])[1]
-            y_bank = bank_tile(b, [P, last - first])
+            first, end = slots_of(groups[0])[0], slots_of(groups[-1])[1]
+            y_bank = bank_tile(b, [P, end - first])
             for group in groups:
                 s0, s1 = slots_of(group)
                 nc.tensor.matmul_mx(
@@ -295,38 +288,36 @@ def tile_moe_pkd_mlp_gelu_kernel(
                     start=True,
                     stop=True,
                 )
-            copy(out=y[:, first:last], in_=y_bank[:])
+            copy(out=y[:, first:end], in_=y_bank[:])
 
         on_scalar, on_vector = nc.scalar.copy, nc.vector.tensor_copy
         expert = [tuple(range(e * TILES, (e + 1) * TILES)) for e in range(E)]
         next_to_last, last = [(j,) for j in expert[E - 1]]
 
+        first_cut = SPLIT[0][1]
         first_layer([0, 1, 2], 0, late=expert[2])
-        first_layer([3], 6, range(2))
-        ident = held("w1_expert3_0", [P, P], F32)
-        nc.scalar.copy(out=ident[:], in_=early_ident[:])
+        first_layer([3], 6, range(first_cut))
+        ident_behind_3 = late_identity(3)
         for j in expert[2]:
             activate(j, accs[j])
-        first_layer([3], 6, range(2, PASSES))
-        for e in range(2):
-            transpose(expert[e], e, ident)
-            copy_turned(expert[e], on_scalar)
+        first_layer([3], 6, range(first_cut, PASSES))
+        turn(expert[0], 0, ident_behind_3, on_scalar)
+        turn(expert[1], 1, ident_behind_3, on_scalar)
         first_layer([4], 2)
-        ident = held(IDENT_BUFFER, [P, P], F32)
-        nc.scalar.copy(out=ident[:], in_=early_ident[:])
-        turn(expert[2], 6, on_scalar)
-        turn(expert[3], 7, on_scalar)
+        ident_behind_4 = late_identity(4)
+        turn(expert[2], 6, ident_behind_4, on_scalar)
+        turn(expert[3], 7, ident_behind_4, on_scalar)
         last_first_layer()
 
         for e in range(4):
             quantize(expert[e])
-        turn(expert[4], 4, on_vector)
-        turn(next_to_last, 0, on_scalar)
-        turn(last, 3, on_scalar)
+        turn(expert[4], 4, ident_behind_4, on_vector)
+        turn(next_to_last, 0, ident_behind_4, on_scalar)
+        turn(last, 3, ident_behind_4, on_scalar)
         quantize(expert[4])
-        second_layer([expert[2], expert[3]], 6, on_scalar)
+        second_layer([expert[2], expert[3]], 5, on_scalar)
         quantize(next_to_last)
-        second_layer([expert[0], expert[1]], 5, on_scalar)
+        second_layer([expert[0], expert[1]], 0, on_scalar)
         quantize(last)
         second_layer([expert[4]], 4, on_vector)
         second_layer([next_to_last, last], 1, on_vector)

@@ -28,6 +28,7 @@ HEAD_EXPERTS = 3
 HEAD = HEAD_EXPERTS * C
 HALF = S // 2
 WIDE_GATHER = HALF // 2
+WINDOW = 1024
 WIDE_PASSES = 2
 WORD_BUFS = 10
 SPLIT, WHOLE = ((0, 2), (2, PASSES)), ((0, PASSES),)
@@ -62,7 +63,7 @@ def tile_moe_pkd_mlp_gelu_kernel(
         pos1_t = lists.tile([P, T // 16], U16, name="pos1_t")
         pos2_t = lists.tile([P, T // 16], U16, name="pos2_t")
 
-        scale_window = held("scale_window", [P, T], U8)
+        scale_window = held("scale_window", [P, WINDOW], U8)
         word_windows = [held("word_window%d" % a, [P, T], I32) for a in range(PASSES)]
         slot_scales = held("slot_scales", [P, S], U8)
         first_planes = [ring_tile([P, 4, HALF], U8), held("first_planes1", [P, 4, HALF], U8)]
@@ -120,7 +121,7 @@ def tile_moe_pkd_mlp_gelu_kernel(
                 )
 
         def gather_scales(g):
-            s0, s1 = g * WIDE_GATHER, (g + 1) * WIDE_GATHER
+            s0, s1 = g * HALF, (g + 1) * HALF
             nc.vector.tensor_copy(slot_scales[:, s0:s1], scale_window[:].indirect(offs_t[:, s0 // 16 : s1 // 16]))
 
         def gather_words(slot_words, s0, s1, a):
@@ -135,15 +136,15 @@ def tile_moe_pkd_mlp_gelu_kernel(
                 gather_words(slot_words[:, s0 : s0 + WIDE_GATHER], s0, s0 + WIDE_GATHER, a)
             head_words.append(slot_words)
 
-        nc.vector.memset(scale_window[64:LAST_ROWS, :].bitcast(I32), 0)
+        nc.vector.memset(scale_window[64:LAST_ROWS, :T].bitcast(I32), 0)
+        nc.vector.memset(scale_window[:, T:].bitcast(I32), 0)
 
         nc.sync.dma_start(offs_t[:], offs)
         nc.scalar.dma_start(
-            out=scale_window[0:64, :].bitcast(I32), in_=x_scales[0:4].rearrange("a f t -> f a t").bitcast(I32)
+            out=scale_window[0:64, :T].bitcast(I32), in_=x_scales[0:4].rearrange("a f t -> f a t").bitcast(I32)
         )
-        nc.scalar.dma_start(out=scale_window[LAST_ROWS:P, :].bitcast(I32), in_=x_scales[PASSES - 1].bitcast(I32))
+        nc.scalar.dma_start(out=scale_window[LAST_ROWS:P, :T].bitcast(I32), in_=x_scales[PASSES - 1].bitcast(I32))
         gather_scales(0)
-        gather_scales(1)
         move_first_planes(nc.scalar, 0)
         load_x(0)
         load_w1_planes(0, (0, 1))
@@ -151,13 +152,12 @@ def tile_moe_pkd_mlp_gelu_kernel(
         make_identity(nc, early_ident[:], nomemset=True)
         load_w1_head(0)
         gather_wide(0)
-        gather_scales(2)
+        gather_scales(1)
         load_w1_planes(0, (2, 3))
         load_x(1)
         load_x(2)
         load_w1_head(1)
         gather_wide(1)
-        gather_scales(3)
         load_x(3)
         load_w1_head(2)
         load_x(4)
@@ -234,15 +234,18 @@ def tile_moe_pkd_mlp_gelu_kernel(
         def last_first_layer():
             for j, tile_banks in zip(range((E - 1) * TILES, E * TILES), LAST_BANKS):
                 width = H // len(tile_banks)
-                for g, b in enumerate(tile_banks):
-                    acc = bank_tile(b, [P, width])
-                    for a in range(PASSES):
-                        if g == 0:
-                            slot_words = ring_tile([P, P], U32)
-                            gather_words(slot_words[:], j * P, (j + 1) * P, a)
-                            tile_words[j, a] = slot_words[:]
-                        first_matmul(acc, j, a, g * width, (g + 1) * width)
-                    activate(j, acc, g * width, (g + 1) * width)
+                group_accs = [bank_tile(b, [P, width]) for b in tile_banks]
+                steps = [(g, a) for g in range(len(tile_banks)) for a in range(PASSES)]
+                if len(tile_banks) > 1:
+                    steps = steps[:4] + steps[5:7] + steps[4:5] + steps[7:]
+                for g, a in steps:
+                    if g == 0:
+                        slot_words = ring_tile([P, P], U32)
+                        gather_words(slot_words[:], j * P, (j + 1) * P, a)
+                        tile_words[j, a] = slot_words[:]
+                    first_matmul(group_accs[g], j, a, g * width, (g + 1) * width)
+                    if a == PASSES - 1:
+                        activate(j, group_accs[g], g * width, (g + 1) * width)
 
         turned = {}
         h_words = {}
@@ -271,7 +274,10 @@ def tile_moe_pkd_mlp_gelu_kernel(
 
         def quantize(group):
             s0, s1 = slots_of(group)
-            h_words[group] = held("h_words%d" % group[0], [P, s1 - s0], U32)
+            if group in expert[:2]:
+                h_words[group] = ring_tile([P, s1 - s0], U32)
+            else:
+                h_words[group] = held("h_words%d" % group[0], [P, s1 - s0], U32)
             nc.vector.quantize_mx(out=h_words[group][:].bitcast(FP8X4), scales=h_plane[:, s0:s1], in_=turned[group][:])
 
         def second_layer(groups, b, copy):

@@ -145,7 +145,6 @@ def tile_moe_pkd_mlp_gelu_kernel(
         )
         nc.scalar.dma_start(out=scale_window[LAST_ROWS:P, :T].bitcast(I32), in_=x_scales[PASSES - 1].bitcast(I32))
         gather_scales(0)
-        move_first_planes(nc.scalar, 0)
         load_x(0)
         load_w1_planes(0, (0, 1))
         nc.vector.memset(early_ident[:], 0.0)
@@ -155,6 +154,7 @@ def tile_moe_pkd_mlp_gelu_kernel(
         gather_scales(1)
         load_w1_planes(0, (2, 3))
         load_x(1)
+        move_first_planes(nc.sync, 0)
         load_x(2)
         load_w1_head(1)
         gather_wide(1)

@@ -113,8 +113,8 @@ def tile_moe_pkd_mlp_gelu_kernel(
                     in_=slot_scales[16 * q : 16 * q + 16, half * HALF : (half + 1) * HALF].bitcast(I32),
                 )
 
-        def move_last_plane():
-            for r in range(4):
+        def move_last_plane(rows):
+            for r in rows:
                 nc.sync.dma_start(
                     out=last_plane[r:P:32, :].bitcast(I32),
                     in_=slot_scales[LAST_ROWS + r : P : 4, :].bitcast(I32),
@@ -153,19 +153,21 @@ def tile_moe_pkd_mlp_gelu_kernel(
         gather_wide(0)
         gather_scales(1)
         load_w1_planes(0, (2, 3))
-        load_x(1)
         move_first_planes(nc.sync, 0)
-        load_x(2)
+        load_x(1)
         load_w1_head(1)
         gather_wide(1)
-        load_x(3)
+        load_x(2)
         load_w1_head(2)
-        load_x(4)
+        load_x(3)
+        move_last_plane((0, 1))
         load_w1_head(3)
-        move_last_plane()
+        move_last_plane((2, 3))
+        load_x(4)
+        load_w1_planes(1, (0, 1))
         load_w1_head(4)
+        load_w1_planes(1, (2, 3))
         move_first_planes(nc.sync, 1)
-        load_w1_planes(1, range(4))
         load_w1_expert(3)
         load_w1_planes(2, range(4))
         load_w1_expert(4)

from contextlib import ExitStack

import concourse.mybir as mybir
from concourse.masks import make_identity

K, T, E, C, H, N = 2560, 768, 6, 256, 512, 128
S = E * C
P = 128
PASSES = K // 512
FLOPS = 2 * S * (K * H + H * N)

F32 = mybir.dt.float32
BF16 = mybir.dt.bfloat16
I32 = mybir.dt.int32
U32 = mybir.dt.uint32
U16 = mybir.dt.uint16
U8 = mybir.dt.uint8
FP8X4 = mybir.dt.float8_e4m3fn_x4
FP4X4 = mybir.dt.float4_e2m1fn_x4
GELU = mybir.ActivationFunctionType.Gelu_apprx_tanh
COPY = mybir.ActivationFunctionType.Copy
MULT = mybir.AluOpType.mult
ADD = mybir.AluOpType.add

ALIGN = 256
TILES = C // P
HEAD_EXPERTS = 3
HEAD = HEAD_EXPERTS * C
HALF = S // 2
WIDE_GATHER = HALF // 2
WINDOW = 1024
WIDE_PASSES = 2
WORD_BUFS = 10
SPLIT, WHOLE = ((0, 2), (2, PASSES)), ((0, PASSES),)
W1_CUTS = {3: SPLIT, 4: SPLIT, 5: WHOLE}
PLANE_SETS = ((0, 3), (3, 4), (4, 6))
LAST_BANKS = ((4,), (6, 5))
QUADS = (0, 2, 1, 3)
LAST_ROWS = P - 16
TOKEN_CUTS = (0, T // 2, T - P, T)


def tile_moe_pkd_mlp_gelu_kernel(
    tc, x_words, x_scales, w1_words, w1_scales, w2_words, w2_scales, gate, offs, pos1, pos2, out
):
    nc = tc.nc
    with ExitStack() as ctx:
        lists = ctx.enter_context(tc.tile_pool(name="lists", bufs=1))
        keep = ctx.enter_context(tc.tile_pool(name="keep", bufs=1))
        word_ring = ctx.enter_context(tc.tile_pool(name="word_ring", bufs=WORD_BUFS))
        banks = ctx.enter_context(tc.psum_pool(name="banks", bufs=1))

        def held(name, shape, dtype):
            return keep.tile(shape, dtype, name=name, align_bytes=ALIGN)

        def ring_tile(shape, dtype):
            return word_ring.tile(shape, dtype, name="ring", align_bytes=ALIGN)

        def bank_tile(b, shape):
            return banks.tile(shape, F32, name="bank%d" % b)

        offs_t = lists.tile([P, S // 16], U16, name="offs_t")
        pos1_t = lists.tile([P, T // 16], U16, name="pos1_t")
        pos2_t = lists.tile([P, T // 16], U16, name="pos2_t")

        scale_window = held("scale_window", [P, WINDOW], U8)
        word_windows = [held("word_window%d" % a, [P, T], I32) for a in range(PASSES)]
        slot_scales = held("slot_scales", [P, S], U8)
        first_planes = [ring_tile([P, 4, HALF], U8), held("first_planes1", [P, 4, HALF], U8)]
        last_plane = held("last_plane", [P, S], U8)
        gates = held("gates", [P, 2, T], F32)
        w2 = held("w2", [P, E, 2 * N], U8)
        h_plane = held("h_plane", [P, S], U8)
        early_ident = held("early_ident", [P, P], F32)
        y = held("y", [P, S], F32)
        w1_planes = [ring_tile([P, HEAD_EXPERTS * PASSES, H], U8)]
        w1_planes.extend(held("w1_planes%d" % e0, [P, (e1 - e0) * PASSES, H], U8) for e0, e1 in PLANE_SETS[1:])
        w2_planes = held("w2_planes", [P, E, N], U8)
        w1_codes = {}

        def load_planes(planes, scales, rows):
            by_row = scales.rearrange("e s (q r) n -> r q (e s) n", r=4)
            for r in rows:
                nc.sync.dma_start(out=planes[r:P:32].bitcast(I32), in_=by_row[r].bitcast(I32))

        def load_w1_planes(plane_set, rows):
            e0, e1 = PLANE_SETS[plane_set]
            load_planes(w1_planes[plane_set], w1_scales[e0:e1], rows)

        def load_x(a):
            nc.sync.dma_start(out=word_windows[a][:], in_=x_words[a].rearrange("p t r -> p (t r)").bitcast(I32))

        def load_w1_head(a):
            shape = [P, HEAD_EXPERTS, 2 * H]
            piece = held("w1_head%d" % a, shape, U8) if a < WIDE_PASSES else ring_tile(shape, U8)
            words = w1_words[0:HEAD_EXPERTS, a].rearrange("e p b -> p e b")
            nc.sync.dma_start(out=piece[:].bitcast(I32), in_=words.bitcast(I32))
            for e in range(HEAD_EXPERTS):
                w1_codes[e, a] = piece[:, e, :]

        def load_w1_expert(e):
            for a0, a1 in W1_CUTS[e]:
                piece = held("w1_expert%d_%d" % (e, a0), [P, a1 - a0, 2 * H], U8)
                words = w1_words[e, a0:a1].rearrange("s p b -> p s b")
                nc.sync.dma_start(out=piece[:].bitcast(I32), in_=words.bitcast(I32))
                for a in range(a0, a1):
                    w1_codes[e, a] = piece[:, a - a0, :]

        def move_first_planes(queue, half):
            for q in QUADS:
                queue.dma_start(
                    out=first_planes[half][32 * q : 32 * q + 4].bitcast(I32),
                    in_=slot_scales[16 * q : 16 * q + 16, half * HALF : (half + 1) * HALF].bitcast(I32),
                )

        def move_last_plane(rows):
            for r in rows:
                nc.sync.dma_start(
                    out=last_plane[r:P:32, :].bitcast(I32),
                    in_=slot_scales[LAST_ROWS + r : P : 4, :].bitcast(I32),
                )

        def gather_scales(g):
            s0, s1 = g * HALF, (g + 1) * HALF
            nc.vector.tensor_copy(slot_scales[:, s0:s1], scale_window[:].indirect(offs_t[:, s0 // 16 : s1 // 16]))

        def gather_words(slot_words, s0, s1, a):
            entries = offs_t[:, s0 // 16 : s1 // 16]
            nc.vector.tensor_copy(slot_words, word_windows[a][:].bitcast(U32).indirect(entries))

        head_words = []

        def gather_wide(a):
            slot_words = held("head_words%d" % a, [P, HEAD], U32)
            for s0 in range(0, HEAD, WIDE_GATHER):
                gather_words(slot_words[:, s0 : s0 + WIDE_GATHER], s0, s0 + WIDE_GATHER, a)
            head_words.append(slot_words)

        nc.vector.memset(scale_window[64:LAST_ROWS, :T].bitcast(I32), 0)
        nc.vector.memset(scale_window[:, T:].bitcast(I32), 0)

        nc.sync.dma_start(offs_t[:], offs)
        nc.scalar.dma_start(
            out=scale_window[0:64, :T].bitcast(I32), in_=x_scales[0:4].rearrange("a f t -> f a t").bitcast(I32)
        )
        nc.scalar.dma_start(out=scale_window[LAST_ROWS:P, :T].bitcast(I32), in_=x_scales[PASSES - 1].bitcast(I32))
        gather_scales(0)
        load_x(0)
        load_w1_planes(0, (0, 1))
        nc.vector.memset(early_ident[:], 0.0)
        make_identity(nc, early_ident[:], nomemset=True)
        load_w1_head(0)
        gather_wide(0)
        gather_scales(1)
        load_w1_planes(0, (2, 3))
        move_first_planes(nc.sync, 0)
        load_x(1)
        load_w1_head(1)
        gather_wide(1)
        load_x(2)
        load_w1_head(2)
        load_x(3)
        move_last_plane((0, 1))
        load_w1_head(3)
        move_last_plane((2, 3))
        load_x(4)
        load_w1_planes(1, (0, 1))
        load_w1_head(4)
        load_w1_planes(1, (2, 3))
        move_first_planes(nc.sync, 1)
        load_w1_expert(3)
        load_w1_planes(2, range(4))
        load_w1_expert(4)
        load_w1_expert(5)
        nc.sync.dma_start(out=w2[:].bitcast(I32), in_=w2_words[:, 0].rearrange("e p b -> p e b").bitcast(I32))
        load_planes(w2_planes, w2_scales, range(4))
        nc.sync.dma_start(pos1_t[:], pos1)
        nc.sync.dma_start(pos2_t[:], pos2)
        nc.sync.dma_start(out=gates[:], in_=gate.rearrange("r p t -> p r t"))

        tile_words = {}
        h = {}

        def gather_pass(experts, a):
            s0 = experts[0] * C
            if s0 == 0 and a < WIDE_PASSES:
                slot_words = head_words[a]
            else:
                slot_words = ring_tile([P, len(experts) * C], U32)
                for e in experts:
                    gather_words(slot_words[:, e * C - s0 : (e + 1) * C - s0], e * C, (e + 1) * C, a)
            for j in range(experts[0] * TILES, (experts[-1] + 1) * TILES):
                tile_words[j, a] = slot_words[:, j * P - s0 : (j + 1) * P - s0]

        def first_matmul(acc, j, a, i0=0, i1=H):
            if a == PASSES - 1:
                token_plane = last_plane[:, j * P : (j + 1) * P]
            else:
                half, s0 = divmod(j * P, HALF)
                token_plane = first_planes[half][:, a, s0 : s0 + P]
            e = j // TILES
            plane_set = sum(e >= e1 for e0, e1 in PLANE_SETS)
            within = e - PLANE_SETS[plane_set][0]
            nc.tensor.matmul_mx(
                out=acc[:],
                lhsT=tile_words[j, a].bitcast(FP8X4),
                lhsT_scale=token_plane,
                rhs=w1_codes[e, a][:, 2 * i0 : 2 * i1].bitcast(FP4X4),
                rhs_scale=w1_planes[plane_set][:, within * PASSES + a, i0:i1],
                start=(a == 0),
                stop=(a == PASSES - 1),
            )

        def activate(j, acc, i0=0, i1=H):
            if i0 == 0:
                h[j] = held("h%d" % j, [P, H], BF16)
            nc.scalar.activation(
                out=h[j][:].rearrange("s (u p d) -> s u p d", u=2, d=2)[:, :, i0 // 4 : i1 // 4],
                in_=acc[:].rearrange("s (p u d) -> s u p d", u=2, d=2),
                func=GELU,
            )

        accs = {}

        def first_layer(experts, first_bank, passes=range(PASSES), late=()):
            tiles = range(experts[0] * TILES, (experts[-1] + 1) * TILES)
            for a in passes:
                gather_pass(experts, a)
                for i, j in enumerate(tiles):
                    if a == 0:
                        accs[j] = bank_tile(first_bank + i, [P, H])
                    first_matmul(accs[j], j, a)
                    if a == PASSES - 1 and j not in late:
                        activate(j, accs[j])

        def last_first_layer():
            for j, tile_banks in zip(range((E - 1) * TILES, E * TILES), LAST_BANKS):
                width = H // len(tile_banks)
                group_accs = [bank_tile(b, [P, width]) for b in tile_banks]
                steps = [(g, a) for g in range(len(tile_banks)) for a in range(PASSES)]
                if len(tile_banks) > 1:
                    steps = steps[:4] + steps[5:7] + steps[4:5] + steps[7:]
                for g, a in steps:
                    if g == 0:
                        slot_words = ring_tile([P, P], U32)
                        gather_words(slot_words[:], j * P, (j + 1) * P, a)
                        tile_words[j, a] = slot_words[:]
                    first_matmul(group_accs[g], j, a, g * width, (g + 1) * width)
                    if a == PASSES - 1:
                        activate(j, group_accs[g], g * width, (g + 1) * width)

        turned = {}
        h_words = {}

        def late_identity(e):
            ident = held("w1_expert%d_0" % e, [P, P], F32)
            nc.scalar.copy(out=ident[:], in_=early_ident[:])
            return ident

        def turn(group, b, ident, copy):
            n = len(group)
            bank = bank_tile(b, [P, n, 2, P])
            for i, j in enumerate(group):
                pairs = h[j][:].bitcast(F32)
                for u in range(2):
                    nc.tensor.transpose(bank[:, i, u, :], pairs[:, u * P : (u + 1) * P], ident[:])
            h_turned = held("h_turned%d" % group[0], [P, n * H], BF16)
            copy(
                out=h_turned[:].bitcast(F32).rearrange("p (i s u) -> p i s u", i=n, u=2),
                in_=bank[:].rearrange("p i u s -> p i s u"),
            )
            turned[group] = h_turned

        def slots_of(group):
            return group[0] * P, (group[-1] + 1) * P

        def quantize(group):
            s0, s1 = slots_of(group)
            if group in expert[:2]:
                h_words[group] = ring_tile([P, s1 - s0], U32)
            else:
                h_words[group] = held("h_words%d" % group[0], [P, s1 - s0], U32)
            nc.vector.quantize_mx(out=h_words[group][:].bitcast(FP8X4), scales=h_plane[:, s0:s1], in_=turned[group][:])

        def second_layer(groups, b, copy):
            first, end = slots_of(groups[0])[0], slots_of(groups[-1])[1]
            y_bank = bank_tile(b, [P, end - first])
            for group in groups:
                s0, s1 = slots_of(group)
                nc.tensor.matmul_mx(
                    out=y_bank[:, s0 - first : s1 - first],
                    lhsT=w2[:, s0 // C, :].bitcast(FP4X4),
                    lhsT_scale=w2_planes[:, s0 // C, :],
                    rhs=h_words[group][:].bitcast(FP8X4),
                    rhs_scale=h_plane[:, s0:s1],
                    start=True,
                    stop=True,
                )
            copy(out=y[:, first:end], in_=y_bank[:])

        on_scalar, on_vector = nc.scalar.copy, nc.vector.tensor_copy
        expert = [tuple(range(e * TILES, (e + 1) * TILES)) for e in range(E)]
        next_to_last, last = [(j,) for j in expert[E - 1]]

        first_cut = SPLIT[0][1]
        first_layer([0, 1, 2], 0, late=expert[2])
        first_layer([3], 6, range(first_cut))
        ident_behind_3 = late_identity(3)
        for j in expert[2]:
            activate(j, accs[j])
        first_layer([3], 6, range(first_cut, PASSES))
        turn(expert[0], 0, ident_behind_3, on_scalar)
        turn(expert[1], 1, ident_behind_3, on_scalar)
        first_layer([4], 2)
        ident_behind_4 = late_identity(4)
        turn(expert[2], 6, ident_behind_4, on_scalar)
        turn(expert[3], 7, ident_behind_4, on_scalar)
        last_first_layer()

        for e in range(4):
            quantize(expert[e])
        turn(expert[4], 4, ident_behind_4, on_vector)
        turn(next_to_last, 0, ident_behind_4, on_scalar)
        turn(last, 3, ident_behind_4, on_scalar)
        quantize(expert[4])
        second_layer([expert[2], expert[3]], 5, on_scalar)
        quantize(next_to_last)
        second_layer([expert[0], expert[1]], 0, on_scalar)
        quantize(last)
        second_layer([expert[4]], 4, on_vector)
        second_layer([next_to_last, last], 1, on_vector)

        pos_t = (pos1_t, pos2_t)

        def entries_of(r, piece):
            t0, t1 = TOKEN_CUTS[piece : piece + 2]
            return y[:].indirect(pos_t[r][:, t0 // 16 : t1 // 16])

        def gate_of(r, piece):
            return gates[:, r, TOKEN_CUTS[piece] : TOKEN_CUTS[piece + 1]]

        def piece_tile(name, r, piece):
            return held("%s%d_%d" % (name, r, piece), [P, TOKEN_CUTS[piece + 1] - TOKEN_CUTS[piece]], F32)

        picked = {}
        weighted = {}

        def fetch_on_scalar(r, piece):
            picked[r, piece] = piece_tile("picked", r, piece)
            nc.scalar.activation(picked[r, piece][:], entries_of(r, piece), COPY)

        def fetch_on_vector(r, piece):
            weighted[r, piece] = piece_tile("weighted", r, piece)
            nc.vector.tensor_tensor(weighted[r, piece][:], entries_of(r, piece), gate_of(r, piece), MULT)

        def weigh(r, piece):
            weighted[r, piece] = piece_tile("weighted", r, piece)
            nc.vector.tensor_tensor(weighted[r, piece][:], picked[r, piece][:], gate_of(r, piece), MULT)

        def add_and_store(queue, piece):
            t0, t1 = TOKEN_CUTS[piece : piece + 2]
            total = held("total%d" % piece, [P, t1 - t0], F32)
            nc.vector.tensor_tensor(total[:], weighted[0, piece][:], weighted[1, piece][:], ADD)
            queue.dma_start(out=out[:, t0:t1], in_=total[:])

        fetch_on_vector(0, 0)
        for r, piece in ((1, 0), (0, 1), (1, 1), (0, 2), (1, 2)):
            fetch_on_scalar(r, piece)
        weigh(1, 0)
        weigh(0, 1)
        add_and_store(nc.sync, 0)
        weigh(1, 1)
        weigh(0, 2)
        weigh(1, 2)
        add_and_store(nc.sync, 1)
        add_and_store(nc.scalar, 2)
